import numpy as np
import ml_dtypes


def mxq(x, axis, fmt="e4m3"):
    dtype, down = {"e4m3": (ml_dtypes.float8_e4m3fn, 7), "e5m2": (ml_dtypes.float8_e5m2, 14)}[fmt]
    v = np.moveaxis(np.asarray(x, np.float32).astype(ml_dtypes.bfloat16).astype(np.float64), axis, -1)
    blocks = v.reshape(v.shape[:-1] + (-1, 32))
    amax = np.abs(blocks).max(-1, keepdims=True)
    byte = np.maximum(np.where(amax > 0, np.frexp(amax)[1] - 1 + 127, 0) - down, 1)
    scale = np.exp2(byte - 127.0)
    codes = (blocks / scale).astype(np.float32).astype(dtype).astype(np.float64)
    return np.moveaxis((codes * scale).reshape(v.shape), -1, axis)


WIDE = False


def mx_kscale(k):
    if not WIDE:
        return np.ones(k)
    levels = np.array([10, -10, 5, -5, 0])
    if k % 512:
        return np.exp2(np.random.permutation(np.resize(levels, k // 32))).repeat(32)
    a = np.empty((k // 512, 16))
    for p in range(k // 512):
        a[p, :8] = np.random.permutation(np.resize(levels, 8))
        for g in range(8):
            far = levels[np.abs(levels - a[p, g]) >= 10]
            a[p, g + 8] = far[np.random.randint(len(far))]
    return np.exp2(a.ravel()).repeat(32)


def f64(x):
    return np.asarray(x).astype(np.float64)


def striped(idx):
    return np.tile(idx.reshape(-1, 16).T, (8, 1)).astype(np.uint16)


def unstriped(offs):
    return offs[:16].T.reshape(-1).astype(np.int64)


def pack_weight(w):
    k, n = w.shape
    w = f64(np.asarray(w, np.float32).astype(ml_dtypes.bfloat16)).reshape(k // 32, 32, n)
    amax = np.abs(w).max(1)
    byte = np.clip(np.where(amax > 0, np.frexp(amax)[1] - 1 + 127 - 7, 1), 1, 254)
    scaled = (w * np.exp2(127.0 - byte)[:, None, :]).reshape(k, n).astype(np.float32)
    words = np.ascontiguousarray(scaled.reshape(k // 512, 128, 4, n).transpose(0, 1, 3, 2)).astype(ml_dtypes.float8_e4m3fn).view(np.uint8)
    return words, np.ascontiguousarray(byte.astype(np.uint8).reshape(k // 512, 16, n))


def unpack_weight(words, scales):
    g, p, n, _ = words.shape
    vals = np.ascontiguousarray(words).view(ml_dtypes.float8_e4m3fn).astype(np.float64) * np.repeat(np.exp2(scales.astype(np.float64) - 127.0), 8, axis=1)[..., None]
    return vals.transpose(0, 1, 3, 2).reshape(g * 512, n)


def relu(v):
    return np.maximum(v, 0.0)


K, T, S, D, V, H, N, U = 512, 4096, 1024, 2, 512, 512, 128, 256
P = 2 ** 7


def setup_inputs():
    n = np.random.standard_normal
    s = mx_kscale(K)[:, None]
    u = mx_kscale(H)
    packed_xT = pack_weight(n((K, T)) * s)
    return {
        "x_words": packed_xT[0],
        "x_scales": packed_xT[1],
        "w1": (n((K, H)) / np.sqrt(K) / s * u).astype(np.float32),
        "w2": (n((H, N)) / np.sqrt(H) / u[:, None]).astype(np.float32),
        "gate": (np.tile(np.random.uniform(0.2, 1.0, (D, 1, V)) / np.sqrt(D), (1, P, 1))).astype(np.float32),
        "gate2": (np.tile(np.random.uniform(0.2, 1.0, (D, 1, U)) / np.sqrt(D), (1, P, 1))).astype(np.float32),
        "offs": striped(np.random.permutation(T)[:S]),
        "pos1": striped(np.random.permutation(S)[:V]),
        "pos2": striped(np.random.permutation(S)[:V]),
        "nxt1": striped(np.random.permutation(V)[:U]),
        "nxt2": striped(np.random.permutation(V)[:U]),
    }


def reference(x_words, x_scales, w1, w2, gate, gate2, offs, pos1, pos2, nxt1, nxt2):
    xq = unpack_weight(x_words, x_scales)[:, unstriped(offs)]
    h = relu(mxq(f64(w1), 0, "e4m3").T @ xq)
    z = h[:, unstriped(pos1)] * f64(gate)[0, :1] + h[:, unstriped(pos2)] * f64(gate)[1, :1]
    g = relu(mxq(f64(w2), 0, "e4m3").T @ mxq(z, 0, "e4m3"))
    return g[:, unstriped(nxt1)] * f64(gate2)[0, :1] + g[:, unstriped(nxt2)] * f64(gate2)[1, :1]

@@ -1,0 +1,178 @@
+from contextlib import ExitStack
+
+import concourse.mybir as mybir
+
+K, T, S, V, H, N, U = 512, 4096, 1024, 512, 512, 128, 256
+FLOPS = 2 * K * H * S + 2 * H * N * V
+
+F32 = mybir.dt.float32
+BF16 = mybir.dt.bfloat16
+I32 = mybir.dt.int32
+U32 = mybir.dt.uint32
+U16 = mybir.dt.uint16
+U8 = mybir.dt.uint8
+FP8X4 = mybir.dt.float8_e4m3fn_x4
+MULT = mybir.AluOpType.mult
+ADD = mybir.AluOpType.add
+RELU = mybir.ActivationFunctionType.Relu
+
+P = 128
+PACK = 4
+STRIPE = 16
+BANK = 512
+V_CHUNKS = ((0, 256), (256, 128), (384, 128))
+
+
+def tile_picked_hop2_relu_p_kernel(
+    tc, x_words, x_scales, w1, w2, gate, gate2, offs, pos1, pos2, nxt1, nxt2, out
+):
+    nc = tc.nc
+    with ExitStack() as ctx:
+        lists = ctx.enter_context(tc.tile_pool(name="lists", bufs=1))
+        keep = ctx.enter_context(tc.tile_pool(name="keep", bufs=1))
+        psum = ctx.enter_context(tc.psum_pool(name="psum", bufs=1))
+
+        def load_list(name, dram, entries):
+            tile = lists.tile([P, entries // STRIPE], U16, name=name)
+            nc.sync.dma_start(tile[:], dram)
+            return tile
+
+        def entries(tile, start, count):
+            return tile[:, start // STRIPE : (start + count) // STRIPE]
+
+        offs_sb = load_list("offs_sb", offs, S)
+        scale_table = keep.tile([P, T], U8, name="scale_table", align_bytes=64)
+        nc.vector.memset(scale_table[:].bitcast(I32), 0)
+        for q in range(4):
+            nc.scalar.dma_start(
+                scale_table[32 * q : 32 * q + 4, :].bitcast(I32),
+                x_scales[0, 4 * q : 4 * q + 4, :].bitcast(I32),
+            )
+        word_table = keep.tile([P, T], U32, name="word_table", align_bytes=64)
+        nc.sync.dma_start(word_table[:].bitcast(I32), x_words[0].rearrange("p n t -> p (n t)").bitcast(I32))
+
+        w1_rows = w1.rearrange("(p j) c -> p j c", j=PACK)
+        half = H // 2
+        w1_raw = []
+        for a in range(2):
+            raw = keep.tile([P, PACK, half], F32, name="w1_raw%d" % a)
+            nc.sync.dma_start(raw[:], w1_rows[:, :, a * half : (a + 1) * half])
+            w1_raw.append(raw)
+        pos_sb = [load_list("pos1_sb", pos1, V), load_list("pos2_sb", pos2, V)]
+        gate_sb = []
+        for d in range(2):
+            g_tile = keep.tile([P, V], F32, name="gate%d" % d)
+            nc.sync.dma_start(g_tile[:], gate[d])
+            gate_sb.append(g_tile)
+        w2_raw = keep.tile([P, PACK, N], F32, name="w2_raw")
+        nc.sync.dma_start(w2_raw[:], w2.rearrange("(p j) n -> p j n", j=PACK))
+        nxt_sb = [load_list("nxt1_sb", nxt1, U), load_list("nxt2_sb", nxt2, U)]
+        gate2_sb = keep.tile([P, 2, U], F32, name="gate2_sb")
+        nc.sync.dma_start(gate2_sb[:], gate2.rearrange("d p u -> p d u"))
+
+        x_scale = keep.tile([P, S], U8, name="x_scale", align_bytes=64)
+        nc.vector.tensor_copy(x_scale[:], scale_table[:].indirect(offs_sb[:]))
+        x_code = []
+        for b in range(S // BANK):
+            code = keep.tile([P, BANK], U32, name="x_code%d" % b, align_bytes=64)
+            nc.vector.tensor_copy(code[:], word_table[:].indirect(entries(offs_sb, b * BANK, BANK)))
+            x_code.append(code)
+
+        w1_bf = keep.tile([P, PACK, P, PACK], BF16, name="w1_bf", align_bytes=64)
+
+        def deal_w1(engine_copy, a, m0, m1):
+            src = w1_raw[a][:].rearrange("p j (m t) -> p m j t", t=PACK)[:, m0:m1, :, :]
+            base = a * (P // 2)
+            dst = w1_bf[:].rearrange("p t m j -> p m j t")[:, base + m0 : base + m1, :, :]
+            engine_copy(dst, src)
+
+        deal_w1(nc.scalar.copy, 0, 0, 64)
+        deal_w1(nc.scalar.copy, 1, 0, 20)
+        deal_w1(nc.vector.tensor_copy, 1, 20, 64)
+        w1_code, w1_scale = [], []
+        for t in range(PACK):
+            code = keep.tile([P, P], U32, name="w1_code%d" % t, align_bytes=64)
+            scale = keep.tile([P, P], U8, name="w1_scale%d" % t, align_bytes=64)
+            nc.vector.quantize_mx(
+                out=code[:].bitcast(FP8X4), scales=scale[:], in_=w1_bf[:, t, :, :].rearrange("p m j -> p (m j)")
+            )
+            w1_code.append(code)
+            w1_scale.append(scale)
+
+        h = []
+        for t in range(PACK):
+            h_t = keep.tile([P, S], F32, name="h%d" % t)
+            for b in range(S // BANK):
+                acc = psum.tile([P, BANK], F32, name="h_acc", tag="h_acc", bufs=6)
+                nc.tensor.matmul_mx(
+                    out=acc[:],
+                    lhsT=w1_code[t][:].bitcast(FP8X4),
+                    lhsT_scale=w1_scale[t][:],
+                    rhs=x_code[b][:].bitcast(FP8X4),
+                    rhs_scale=x_scale[:, b * BANK : (b + 1) * BANK],
+                    start=True,
+                    stop=True,
+                )
+                cols = h_t[:, b * BANK : (b + 1) * BANK]
+                if t == 0 and b == 1:
+                    nc.vector.tensor_scalar_max(cols, acc[:], 0.0)
+                else:
+                    nc.scalar.activation(cols, acc[:], RELU)
+            h.append(h_t)
+
+        w2_bf = keep.tile([P, N, PACK], BF16, name="w2_bf", align_bytes=64)
+        nc.scalar.copy(
+            w2_bf[:].rearrange("p (c i) j -> p c j i", i=PACK),
+            w2_raw[:].rearrange("p j (c i) -> p c j i", i=PACK),
+        )
+        w2_code = keep.tile([P, N], U32, name="w2_code", align_bytes=64)
+        w2_scale = keep.tile([P, N], U8, name="w2_scale", align_bytes=64)
+        nc.vector.quantize_mx(
+            out=w2_code[:].bitcast(FP8X4), scales=w2_scale[:], in_=w2_bf[:].rearrange("p n j -> p (n j)")
+        )
+
+        g = keep.tile([P, V], F32, name="g")
+        for c, (v0, width) in enumerate(V_CHUNKS):
+            terms = []
+            for d in range(2):
+                terms.append(keep.tile([P, PACK, width], F32, name="term%d_%d" % (c, d)))
+            for t in range(PACK):
+                for d in range(2):
+                    nc.vector.tensor_tensor(
+                        terms[d][:, t, :],
+                        h[t][:].indirect(entries(pos_sb[d], v0, width)),
+                        gate_sb[d][:, v0 : v0 + width],
+                        MULT,
+                    )
+            z_bf = keep.tile([P, width, PACK], BF16, name="z_bf%d" % c, align_bytes=64)
+            nc.vector.tensor_tensor(
+                z_bf[:].rearrange("p (c i) t -> p c t i", i=PACK),
+                terms[0][:].rearrange("p t (c i) -> p c t i", i=PACK),
+                terms[1][:].rearrange("p t (c i) -> p c t i", i=PACK),
+                ADD,
+            )
+            z_code = keep.tile([P, width], U32, name="z_code%d" % c, align_bytes=64)
+            z_scale = keep.tile([P, width], U8, name="z_scale%d" % c, align_bytes=64)
+            nc.vector.quantize_mx(
+                out=z_code[:].bitcast(FP8X4), scales=z_scale[:], in_=z_bf[:].rearrange("p v t -> p (v t)")
+            )
+            g_acc = psum.tile([P, width], F32, name="g_acc", tag="g_acc%d" % (c % 2))
+            nc.tensor.matmul_mx(
+                out=g_acc[:],
+                lhsT=w2_code[:].bitcast(FP8X4),
+                lhsT_scale=w2_scale[:],
+                rhs=z_code[:].bitcast(FP8X4),
+                rhs_scale=z_scale[:],
+                start=True,
+                stop=True,
+            )
+            nc.scalar.activation(g[:, v0 : v0 + width], g_acc[:], RELU)
+
+        last = []
+        for d in range(2):
+            term = keep.tile([P, U], F32, name="root_term%d" % d)
+            nc.vector.tensor_tensor(term[:], g[:].indirect(nxt_sb[d][:]), gate2_sb[:, d, :], MULT)
+            last.append(term)
+        result = keep.tile([P, U], F32, name="result")
+        nc.vector.tensor_tensor(result[:], last[0][:], last[1][:], ADD)
+        nc.sync.dma_start(out, result[:])

@@ -1,6 +1,7 @@
 from contextlib import ExitStack
 
 import concourse.mybir as mybir
+from concourse.masks import make_identity
 
 K, T, S, V, H, N, U = 512, 4096, 1024, 512, 512, 128, 256
 FLOPS = 2 * K * H * S + 2 * H * N * V
@@ -41,13 +42,9 @@ def tile_picked_hop2_relu_p_kernel(
             return tile[:, start // STRIPE : (start + count) // STRIPE]
 
         offs_sb = load_list("offs_sb", offs, S)
-        scale_table = keep.tile([P, T], U8, name="scale_table", align_bytes=64)
+        scale_table = keep.tile([P, T], U8, name="scale_table", tag="in_turn", align_bytes=64)
         nc.vector.memset(scale_table[:].bitcast(I32), 0)
-        for q in range(4):
-            nc.scalar.dma_start(
-                scale_table[32 * q : 32 * q + 4, :].bitcast(I32),
-                x_scales[0, 4 * q : 4 * q + 4, :].bitcast(I32),
-            )
+        nc.scalar.dma_start(scale_table[0:P:8, :].bitcast(I32), x_scales[0].bitcast(I32))
         word_table = keep.tile([P, T], U32, name="word_table", align_bytes=64)
         nc.sync.dma_start(word_table[:].bitcast(I32), x_words[0].rearrange("p n t -> p (n t)").bitcast(I32))
 
@@ -59,11 +56,8 @@ def tile_picked_hop2_relu_p_kernel(
             nc.sync.dma_start(raw[:], w1_rows[:, :, a * half : (a + 1) * half])
             w1_raw.append(raw)
         pos_sb = [load_list("pos1_sb", pos1, V), load_list("pos2_sb", pos2, V)]
-        gate_sb = []
-        for d in range(2):
-            g_tile = keep.tile([P, V], F32, name="gate%d" % d)
-            nc.sync.dma_start(g_tile[:], gate[d])
-            gate_sb.append(g_tile)
+        gate_sb = keep.tile([P, 2, V], F32, name="gate_sb")
+        nc.sync.dma_start(gate_sb[:], gate.rearrange("d p v -> p d v"))
         w2_raw = keep.tile([P, PACK, N], F32, name="w2_raw")
         nc.sync.dma_start(w2_raw[:], w2.rearrange("(p j) n -> p j n", j=PACK))
         nxt_sb = [load_list("nxt1_sb", nxt1, U), load_list("nxt2_sb", nxt2, U)]
@@ -71,12 +65,22 @@ def tile_picked_hop2_relu_p_kernel(
         nc.sync.dma_start(gate2_sb[:], gate2.rearrange("d p u -> p d u"))
 
         x_scale = keep.tile([P, S], U8, name="x_scale", align_bytes=64)
-        nc.vector.tensor_copy(x_scale[:], scale_table[:].indirect(offs_sb[:]))
-        x_code = []
+        nc.vector.memset(x_scale[:].bitcast(I32), 0)
+        ident = keep.tile([P, P], F32, name="ident")
+        make_identity(nc, ident[:])
+        warm = keep.tile([P, 16], F32, name="warm")
+        nc.vector.memset(warm[:, 0:8], 0.0)
+        nc.scalar.activation(warm[:, 8:16], warm[:, 0:8], RELU)
+
+        picked_scale = keep.tile([P, S], U8, name="picked_scale", align_bytes=64)
+        nc.vector.tensor_copy(picked_scale[:], scale_table[:].indirect(offs_sb[:]))
+        for r in range(4):
+            nc.scalar.dma_start(x_scale[r:P:32, :].bitcast(I32), picked_scale[8 * r : P : 32, :].bitcast(I32))
+        x_code = keep.tile([P, S], U32, name="x_code", tag="in_turn", align_bytes=64)
         for b in range(S // BANK):
-            code = keep.tile([P, BANK], U32, name="x_code%d" % b, align_bytes=64)
-            nc.vector.tensor_copy(code[:], word_table[:].indirect(entries(offs_sb, b * BANK, BANK)))
-            x_code.append(code)
+            nc.vector.tensor_copy(
+                x_code[:, b * BANK : (b + 1) * BANK], word_table[:].indirect(entries(offs_sb, b * BANK, BANK))
+            )
 
         w1_bf = keep.tile([P, PACK, P, PACK], BF16, name="w1_bf", align_bytes=64)
 
@@ -103,12 +107,12 @@ def tile_picked_hop2_relu_p_kernel(
         for t in range(PACK):
             h_t = keep.tile([P, S], F32, name="h%d" % t)
             for b in range(S // BANK):
-                acc = psum.tile([P, BANK], F32, name="h_acc", tag="h_acc", bufs=6)
+                acc = psum.tile([P, BANK], F32, name="h_acc", tag="acc", bufs=5)
                 nc.tensor.matmul_mx(
                     out=acc[:],
                     lhsT=w1_code[t][:].bitcast(FP8X4),
                     lhsT_scale=w1_scale[t][:],
-                    rhs=x_code[b][:].bitcast(FP8X4),
+                    rhs=x_code[:, b * BANK : (b + 1) * BANK].bitcast(FP8X4),
                     rhs_scale=x_scale[:, b * BANK : (b + 1) * BANK],
                     start=True,
                     stop=True,
@@ -120,7 +124,7 @@ def tile_picked_hop2_relu_p_kernel(
                     nc.scalar.activation(cols, acc[:], RELU)
             h.append(h_t)
 
-        w2_bf = keep.tile([P, N, PACK], BF16, name="w2_bf", align_bytes=64)
+        w2_bf = keep.tile([P, N, PACK], BF16, name="w2_bf", tag="in_turn", align_bytes=64)
         nc.scalar.copy(
             w2_bf[:].rearrange("p (c i) j -> p c j i", i=PACK),
             w2_raw[:].rearrange("p j (c i) -> p c j i", i=PACK),
@@ -133,30 +137,64 @@ def tile_picked_hop2_relu_p_kernel(
 
         g = keep.tile([P, V], F32, name="g")
         for c, (v0, width) in enumerate(V_CHUNKS):
-            terms = []
+            terms = {}
             for d in range(2):
-                terms.append(keep.tile([P, PACK, width], F32, name="term%d_%d" % (c, d)))
+                if c == 0:
+                    for t in range(PACK):
+                        own = keep.tile([P, width], F32, name="term0_%d_%d" % (t, d), tag="term%d_%d" % (t, d))
+                        terms[d, t] = own[:]
+                else:
+                    joint = keep.tile([P, PACK, width], F32, name="term%d_%d" % (c, d), tag="term%d_%d" % (c + 1, d))
+                    terms[d] = joint
+                    for t in range(PACK):
+                        terms[d, t] = joint[:, t, :]
             for t in range(PACK):
                 for d in range(2):
                     nc.vector.tensor_tensor(
-                        terms[d][:, t, :],
+                        terms[d, t],
                         h[t][:].indirect(entries(pos_sb[d], v0, width)),
-                        gate_sb[d][:, v0 : v0 + width],
+                        gate_sb[:, d, v0 : v0 + width],
                         MULT,
                     )
-            z_bf = keep.tile([P, width, PACK], BF16, name="z_bf%d" % c, align_bytes=64)
-            nc.vector.tensor_tensor(
-                z_bf[:].rearrange("p (c i) t -> p c t i", i=PACK),
-                terms[0][:].rearrange("p t (c i) -> p c t i", i=PACK),
-                terms[1][:].rearrange("p t (c i) -> p c t i", i=PACK),
-                ADD,
-            )
-            z_code = keep.tile([P, width], U32, name="z_code%d" % c, align_bytes=64)
+            z_bf = keep.tile([P, width, PACK], BF16, name="z_bf%d" % c, tag="z_bf%d" % (c % 2), align_bytes=64)
+            if c == len(V_CHUNKS) - 1:
+                nc.vector.tensor_tensor(
+                    z_bf[:].rearrange("p (c i) t -> p c t i", i=PACK),
+                    terms[0][:].rearrange("p t (c i) -> p c t i", i=PACK),
+                    terms[1][:].rearrange("p t (c i) -> p c t i", i=PACK),
+                    ADD,
+                )
+            else:
+                blocks = width // P
+                sums = [psum.tile([P, PACK, P], F32, name="z_sum", tag="z_sum", bufs=2) for blk in range(blocks)]
+                for t in range(PACK):
+                    for blk in range(blocks):
+                        for d in range(2):
+                            nc.tensor.matmul(
+                                sums[blk][:, t, :],
+                                terms[d, t][:, blk * P : (blk + 1) * P],
+                                ident[:],
+                                start=(d == 0),
+                                stop=(d == 1),
+                                is_transpose=True,
+                            )
+                back = psum.tile([P, blocks, 2, P], F32, name="z_back", tag="z_back")
+                for blk in range(blocks):
+                    z_rows = keep.tile([P, 2, P, 2], BF16, name="z_rows%d_%d" % (c, blk))
+                    nc.scalar.copy(z_rows[:], sums[blk][:].rearrange("v (u e) p -> v u p e", e=2))
+                    pairs = z_rows[:].rearrange("v u p e -> v (u p e)").bitcast(F32)
+                    for u in range(2):
+                        nc.tensor.transpose(back[:, blk, u, :], pairs[:, u * P : (u + 1) * P], ident[:])
+                nc.scalar.copy(
+                    z_bf[:].rearrange("p v t -> p (v t)").bitcast(F32).rearrange("p (b v u) -> p b v u", b=blocks, u=2),
+                    back[:].rearrange("p b u v -> p b v u"),
+                )
+            z_code = keep.tile([P, width], U32, name="z_code%d" % c, tag="z_bf1" if c == 2 else "z_code%d" % c, align_bytes=64)
             z_scale = keep.tile([P, width], U8, name="z_scale%d" % c, align_bytes=64)
             nc.vector.quantize_mx(
                 out=z_code[:].bitcast(FP8X4), scales=z_scale[:], in_=z_bf[:].rearrange("p v t -> p (v t)")
             )
-            g_acc = psum.tile([P, width], F32, name="g_acc", tag="g_acc%d" % (c % 2))
+            g_acc = psum.tile([P, width], F32, name="g_acc", tag="acc", bufs=5)
             nc.tensor.matmul_mx(
                 out=g_acc[:],
                 lhsT=w2_code[:].bitcast(FP8X4),
@@ -168,11 +206,15 @@ def tile_picked_hop2_relu_p_kernel(
             )
             nc.scalar.activation(g[:, v0 : v0 + width], g_acc[:], RELU)
 
-        last = []
-        for d in range(2):
-            term = keep.tile([P, U], F32, name="root_term%d" % d)
-            nc.vector.tensor_tensor(term[:], g[:].indirect(nxt_sb[d][:]), gate2_sb[:, d, :], MULT)
-            last.append(term)
-        result = keep.tile([P, U], F32, name="result")
-        nc.vector.tensor_tensor(result[:], last[0][:], last[1][:], ADD)
-        nc.sync.dma_start(out, result[:])
+        for a in range(2):
+            r0, count = a * U // 2, U // 2
+            last = []
+            for d in range(2):
+                term = keep.tile([P, count], F32, name="root_term%d_%d" % (a, d))
+                nc.vector.tensor_tensor(
+                    term[:], g[:].indirect(entries(nxt_sb[d], r0, count)), gate2_sb[:, d, r0 : r0 + count], MULT
+                )
+                last.append(term)
+            result = keep.tile([P, count], F32, name="result%d" % a)
+            nc.vector.tensor_tensor(result[:], last[0][:], last[1][:], ADD)
+            nc.sync.dma_start(out[:, r0 : r0 + count], result[:])

@@ -21,6 +21,7 @@ P = 128
 PACK = 4
 STRIPE = 16
 BANK = 512
+X_LEAD = 768
 V_CHUNKS = ((0, 256), (256, 128), (384, 128))
 
 
@@ -42,40 +43,39 @@ def tile_picked_hop2_relu_p_kernel(
             return tile[:, start // STRIPE : (start + count) // STRIPE]
 
         offs_sb = load_list("offs_sb", offs, S)
+        word_table = keep.tile([P, T], U32, name="word_table", align_bytes=64)
+        word_rows = x_words[0].rearrange("p n t -> p (n t)").bitcast(I32)
+        nc.sync.dma_start(word_table[:, :X_LEAD].bitcast(I32), word_rows[:, :X_LEAD])
         scale_table = keep.tile([P, T], U8, name="scale_table", tag="in_turn", align_bytes=64)
         nc.vector.memset(scale_table[:].bitcast(I32), 0)
-        nc.scalar.dma_start(scale_table[0:P:8, :].bitcast(I32), x_scales[0].bitcast(I32))
-        word_table = keep.tile([P, T], U32, name="word_table", align_bytes=64)
-        nc.sync.dma_start(word_table[:].bitcast(I32), x_words[0].rearrange("p n t -> p (n t)").bitcast(I32))
+        nc.sync.dma_start(scale_table[0:P:8, :].bitcast(I32), x_scales[0].bitcast(I32))
+        nc.sync.dma_start(word_table[:, X_LEAD:].bitcast(I32), word_rows[:, X_LEAD:])
 
         w1_rows = w1.rearrange("(p j) c -> p j c", j=PACK)
         half = H // 2
-        w1_raw = []
-        for a in range(2):
-            raw = keep.tile([P, PACK, half], F32, name="w1_raw%d" % a)
-            nc.sync.dma_start(raw[:], w1_rows[:, :, a * half : (a + 1) * half])
-            w1_raw.append(raw)
-        pos_sb = [load_list("pos1_sb", pos1, V), load_list("pos2_sb", pos2, V)]
+        w1_raw = [keep.tile([P, PACK, half], F32, name="w1_raw%d" % a) for a in range(2)]
+        nc.sync.dma_start(w1_raw[0][:], w1_rows[:, :, :half])
+        nc.sync.dma_start(w1_raw[1][:], w1_rows[:, :, half:])
+
+        x_scale = keep.tile([P, S], U8, name="x_scale", align_bytes=64)
+        nc.vector.memset(x_scale[:].bitcast(I32), 0)
+        picked_scale = keep.tile([P, S], U8, name="picked_scale", align_bytes=64)
+        nc.vector.tensor_copy(picked_scale[:], scale_table[:].indirect(offs_sb[:]))
+        for r in range(4):
+            nc.sync.dma_start(x_scale[r:P:32, :].bitcast(I32), picked_scale[8 * r : P : 32, :].bitcast(I32))
+
         gate_sb = keep.tile([P, 2, V], F32, name="gate_sb")
         nc.sync.dma_start(gate_sb[:], gate.rearrange("d p v -> p d v"))
+        pos_sb = [load_list("pos1_sb", pos1, V), load_list("pos2_sb", pos2, V)]
         w2_raw = keep.tile([P, PACK, N], F32, name="w2_raw")
         nc.sync.dma_start(w2_raw[:], w2.rearrange("(p j) n -> p j n", j=PACK))
         nxt_sb = [load_list("nxt1_sb", nxt1, U), load_list("nxt2_sb", nxt2, U)]
         gate2_sb = keep.tile([P, 2, U], F32, name="gate2_sb")
         nc.sync.dma_start(gate2_sb[:], gate2.rearrange("d p u -> p d u"))
 
-        x_scale = keep.tile([P, S], U8, name="x_scale", align_bytes=64)
-        nc.vector.memset(x_scale[:].bitcast(I32), 0)
         ident = keep.tile([P, P], F32, name="ident")
         make_identity(nc, ident[:])
-        warm = keep.tile([P, 16], F32, name="warm")
-        nc.vector.memset(warm[:, 0:8], 0.0)
-        nc.scalar.activation(warm[:, 8:16], warm[:, 0:8], RELU)
 
-        picked_scale = keep.tile([P, S], U8, name="picked_scale", align_bytes=64)
-        nc.vector.tensor_copy(picked_scale[:], scale_table[:].indirect(offs_sb[:]))
-        for r in range(4):
-            nc.scalar.dma_start(x_scale[r:P:32, :].bitcast(I32), picked_scale[8 * r : P : 32, :].bitcast(I32))
         x_code = keep.tile([P, S], U32, name="x_code", tag="in_turn", align_bytes=64)
         for b in range(S // BANK):
             nc.vector.tensor_copy(
@@ -85,9 +85,9 @@ def tile_picked_hop2_relu_p_kernel(
         w1_bf = keep.tile([P, PACK, P, PACK], BF16, name="w1_bf", align_bytes=64)
 
         def deal_w1(engine_copy, a, m0, m1):
-            src = w1_raw[a][:].rearrange("p j (m t) -> p m j t", t=PACK)[:, m0:m1, :, :]
+            src = w1_raw[a][:].rearrange("p j (m t) -> p m t j", t=PACK)[:, m0:m1, :, :]
             base = a * (P // 2)
-            dst = w1_bf[:].rearrange("p t m j -> p m j t")[:, base + m0 : base + m1, :, :]
+            dst = w1_bf[:].rearrange("p t m j -> p m t j")[:, base + m0 : base + m1, :, :]
             engine_copy(dst, src)
 
         deal_w1(nc.scalar.copy, 0, 0, 64)
@@ -106,19 +106,20 @@ def tile_picked_hop2_relu_p_kernel(
         h = []
         for t in range(PACK):
             h_t = keep.tile([P, S], F32, name="h%d" % t)
-            for b in range(S // BANK):
-                acc = psum.tile([P, BANK], F32, name="h_acc", tag="acc", bufs=5)
+            pieces = ((0, BANK), (BANK, BANK // 2), (3 * BANK // 2, BANK // 2)) if t == 0 else ((0, BANK), (BANK, BANK))
+            for s0, count in pieces:
+                acc = psum.tile([P, count], F32, name="h_acc", tag="acc", bufs=5)
                 nc.tensor.matmul_mx(
                     out=acc[:],
                     lhsT=w1_code[t][:].bitcast(FP8X4),
                     lhsT_scale=w1_scale[t][:],
-                    rhs=x_code[:, b * BANK : (b + 1) * BANK].bitcast(FP8X4),
-                    rhs_scale=x_scale[:, b * BANK : (b + 1) * BANK],
+                    rhs=x_code[:, s0 : s0 + count].bitcast(FP8X4),
+                    rhs_scale=x_scale[:, s0 : s0 + count],
                     start=True,
                     stop=True,
                 )
-                cols = h_t[:, b * BANK : (b + 1) * BANK]
-                if t == 0 and b == 1:
+                cols = h_t[:, s0 : s0 + count]
+                if count < BANK:
                     nc.vector.tensor_scalar_max(cols, acc[:], 0.0)
                 else:
                     nc.scalar.activation(cols, acc[:], RELU)
@@ -126,8 +127,8 @@ def tile_picked_hop2_relu_p_kernel(
 
         w2_bf = keep.tile([P, N, PACK], BF16, name="w2_bf", tag="in_turn", align_bytes=64)
         nc.scalar.copy(
-            w2_bf[:].rearrange("p (c i) j -> p c j i", i=PACK),
-            w2_raw[:].rearrange("p j (c i) -> p c j i", i=PACK),
+            w2_bf[:].rearrange("p (c i) j -> p c j i", i=2),
+            w2_raw[:].rearrange("p j (c i) -> p c j i", i=2),
         )
         w2_code = keep.tile([P, N], U32, name="w2_code", align_bytes=64)
         w2_scale = keep.tile([P, N], U8, name="w2_scale", align_bytes=64)
@@ -159,9 +160,9 @@ def tile_picked_hop2_relu_p_kernel(
             z_bf = keep.tile([P, width, PACK], BF16, name="z_bf%d" % c, tag="z_bf%d" % (c % 2), align_bytes=64)
             if c == len(V_CHUNKS) - 1:
                 nc.vector.tensor_tensor(
-                    z_bf[:].rearrange("p (c i) t -> p c t i", i=PACK),
-                    terms[0][:].rearrange("p t (c i) -> p c t i", i=PACK),
-                    terms[1][:].rearrange("p t (c i) -> p c t i", i=PACK),
+                    z_bf[:].rearrange("p (c i) t -> p c t i", i=2),
+                    terms[0][:].rearrange("p t (c i) -> p c t i", i=2),
+                    terms[1][:].rearrange("p t (c i) -> p c t i", i=2),
                     ADD,
                 )
             else:

@@ -19,10 +19,17 @@ RELU = mybir.ActivationFunctionType.Relu
 
 P = 128
 PACK = 4
+HOPS = 2
 STRIPE = 16
+QUADRANT = 32
+SCALE_STEP = 8
 BANK = 512
-X_LEAD = 768
-V_CHUNKS = ((0, 256), (256, 128), (384, 128))
+BANKS = 8
+
+X_LEAD = 1024
+TURNED = 384
+FIRST_PIECES = ((0, 256), (256, 256), (512, 256), (768, 128), (896, 128))
+Z_GROUPS = ((0, 256), (256, 128), (TURNED, V - TURNED))
 
 
 def tile_picked_hop2_relu_p_kernel(
@@ -34,21 +41,28 @@ def tile_picked_hop2_relu_p_kernel(
         keep = ctx.enter_context(tc.tile_pool(name="keep", bufs=1))
         psum = ctx.enter_context(tc.psum_pool(name="psum", bufs=1))
 
-        def load_list(name, dram, entries):
-            tile = lists.tile([P, entries // STRIPE], U16, name=name)
+        taken = []
+
+        def bank_tile(shape, name):
+            taken.append(name)
+            return psum.tile(shape, F32, name=name, tag="bank%d" % (len(taken) % BANKS))
+
+        def load_list(name, dram, count):
+            tile = lists.tile([P, count // STRIPE], U16, name=name)
             nc.sync.dma_start(tile[:], dram)
             return tile
 
         def entries(tile, start, count):
             return tile[:, start // STRIPE : (start + count) // STRIPE]
 
-        offs_sb = load_list("offs_sb", offs, S)
         word_table = keep.tile([P, T], U32, name="word_table", align_bytes=64)
         word_rows = x_words[0].rearrange("p n t -> p (n t)").bitcast(I32)
         nc.sync.dma_start(word_table[:, :X_LEAD].bitcast(I32), word_rows[:, :X_LEAD])
+        offs_sb = load_list("offs_sb", offs, S)
+
         scale_table = keep.tile([P, T], U8, name="scale_table", tag="in_turn", align_bytes=64)
         nc.vector.memset(scale_table[:].bitcast(I32), 0)
-        nc.sync.dma_start(scale_table[0:P:8, :].bitcast(I32), x_scales[0].bitcast(I32))
+        nc.sync.dma_start(scale_table[0:P:SCALE_STEP, :].bitcast(I32), x_scales[0].bitcast(I32))
         nc.sync.dma_start(word_table[:, X_LEAD:].bitcast(I32), word_rows[:, X_LEAD:])
 
         w1_rows = w1.rearrange("(p j) c -> p j c", j=PACK)
@@ -61,38 +75,36 @@ def tile_picked_hop2_relu_p_kernel(
         nc.vector.memset(x_scale[:].bitcast(I32), 0)
         picked_scale = keep.tile([P, S], U8, name="picked_scale", align_bytes=64)
         nc.vector.tensor_copy(picked_scale[:], scale_table[:].indirect(offs_sb[:]))
-        for r in range(4):
-            nc.sync.dma_start(x_scale[r:P:32, :].bitcast(I32), picked_scale[8 * r : P : 32, :].bitcast(I32))
+        for r in range(QUADRANT // SCALE_STEP):
+            nc.sync.dma_start(
+                x_scale[r:P:QUADRANT, :].bitcast(I32), picked_scale[SCALE_STEP * r : P : QUADRANT, :].bitcast(I32)
+            )
 
-        gate_sb = keep.tile([P, 2, V], F32, name="gate_sb")
+        gate_sb = keep.tile([P, HOPS, V], F32, name="gate_sb")
         nc.sync.dma_start(gate_sb[:], gate.rearrange("d p v -> p d v"))
         pos_sb = [load_list("pos1_sb", pos1, V), load_list("pos2_sb", pos2, V)]
         w2_raw = keep.tile([P, PACK, N], F32, name="w2_raw")
         nc.sync.dma_start(w2_raw[:], w2.rearrange("(p j) n -> p j n", j=PACK))
         nxt_sb = [load_list("nxt1_sb", nxt1, U), load_list("nxt2_sb", nxt2, U)]
-        gate2_sb = keep.tile([P, 2, U], F32, name="gate2_sb")
+        gate2_sb = keep.tile([P, HOPS, U], F32, name="gate2_sb")
         nc.sync.dma_start(gate2_sb[:], gate2.rearrange("d p u -> p d u"))
 
         ident = keep.tile([P, P], F32, name="ident")
         make_identity(nc, ident[:])
 
         x_code = keep.tile([P, S], U32, name="x_code", tag="in_turn", align_bytes=64)
-        for b in range(S // BANK):
-            nc.vector.tensor_copy(
-                x_code[:, b * BANK : (b + 1) * BANK], word_table[:].indirect(entries(offs_sb, b * BANK, BANK))
-            )
+        nc.vector.tensor_copy(x_code[:], word_table[:].indirect(offs_sb[:]))
 
         w1_bf = keep.tile([P, PACK, P, PACK], BF16, name="w1_bf", align_bytes=64)
 
-        def deal_w1(engine_copy, a, m0, m1):
-            src = w1_raw[a][:].rearrange("p j (m t) -> p m t j", t=PACK)[:, m0:m1, :, :]
-            base = a * (P // 2)
-            dst = w1_bf[:].rearrange("p t m j -> p m t j")[:, base + m0 : base + m1, :, :]
+        def deal_w1(engine_copy, a, t0, t1):
+            src = w1_raw[a][:].rearrange("p j (m t) -> p m t j", t=PACK)[:, :, t0:t1, :]
+            dst = w1_bf[:].rearrange("p t m j -> p m t j")[:, a * P // 2 : (a + 1) * P // 2, t0:t1, :]
             engine_copy(dst, src)
 
-        deal_w1(nc.scalar.copy, 0, 0, 64)
-        deal_w1(nc.scalar.copy, 1, 0, 20)
-        deal_w1(nc.vector.tensor_copy, 1, 20, 64)
+        deal_w1(nc.scalar.copy, 0, 0, PACK)
+        deal_w1(nc.vector.tensor_copy, 1, 0, PACK // 2)
+        deal_w1(nc.scalar.copy, 1, PACK // 2, PACK)
         w1_code, w1_scale = [], []
         for t in range(PACK):
             code = keep.tile([P, P], U32, name="w1_code%d" % t, align_bytes=64)
@@ -106,9 +118,9 @@ def tile_picked_hop2_relu_p_kernel(
         h = []
         for t in range(PACK):
             h_t = keep.tile([P, S], F32, name="h%d" % t)
-            pieces = ((0, BANK), (BANK, BANK // 2), (3 * BANK // 2, BANK // 2)) if t == 0 else ((0, BANK), (BANK, BANK))
-            for s0, count in pieces:
-                acc = psum.tile([P, count], F32, name="h_acc", tag="acc", bufs=5)
+            pieces = FIRST_PIECES if t == 0 else ((0, BANK), (BANK, BANK))
+            for n, (s0, count) in enumerate(pieces):
+                acc = bank_tile([P, count], "h_acc")
                 nc.tensor.matmul_mx(
                     out=acc[:],
                     lhsT=w1_code[t][:].bitcast(FP8X4),
@@ -119,7 +131,7 @@ def tile_picked_hop2_relu_p_kernel(
                     stop=True,
                 )
                 cols = h_t[:, s0 : s0 + count]
-                if count < BANK:
+                if t == 0 and n % 2 == 1:
                     nc.vector.tensor_scalar_max(cols, acc[:], 0.0)
                 else:
                     nc.scalar.activation(cols, acc[:], RELU)
@@ -136,66 +148,69 @@ def tile_picked_hop2_relu_p_kernel(
             out=w2_code[:].bitcast(FP8X4), scales=w2_scale[:], in_=w2_bf[:].rearrange("p n j -> p (n j)")
         )
 
-        g = keep.tile([P, V], F32, name="g")
-        for c, (v0, width) in enumerate(V_CHUNKS):
-            terms = {}
-            for d in range(2):
-                if c == 0:
-                    for t in range(PACK):
-                        own = keep.tile([P, width], F32, name="term0_%d_%d" % (t, d), tag="term%d_%d" % (t, d))
-                        terms[d, t] = own[:]
-                else:
-                    joint = keep.tile([P, PACK, width], F32, name="term%d_%d" % (c, d), tag="term%d_%d" % (c + 1, d))
-                    terms[d] = joint
-                    for t in range(PACK):
-                        terms[d, t] = joint[:, t, :]
-            for t in range(PACK):
-                for d in range(2):
-                    nc.vector.tensor_tensor(
-                        terms[d, t],
-                        h[t][:].indirect(entries(pos_sb[d], v0, width)),
-                        gate_sb[:, d, v0 : v0 + width],
-                        MULT,
+        def gather_term(dst, t, d, v0, width):
+            nc.vector.tensor_tensor(
+                dst, h[t][:].indirect(entries(pos_sb[d], v0, width)), gate_sb[:, d, v0 : v0 + width], MULT
+            )
+
+        sums = [bank_tile([P, PACK, P], "z_sum") for blk in range(TURNED // P)]
+        backs = [bank_tile([P, width // P, 2, P], "z_back") for v0, width in Z_GROUPS[:-1]]
+        back_of = [backs[c][:, b, :, :] for c, (v0, width) in enumerate(Z_GROUPS[:-1]) for b in range(width // P)]
+        for t in range(PACK):
+            early = []
+            for d in range(HOPS):
+                term = keep.tile([P, TURNED], F32, name="early%d_%d" % (t, d), tag="term%d_%d" % (t, d))
+                gather_term(term[:], t, d, 0, TURNED)
+                early.append(term)
+            for blk in range(TURNED // P):
+                for d in range(HOPS):
+                    nc.tensor.matmul(
+                        sums[blk][:, t, :],
+                        early[d][:, blk * P : (blk + 1) * P],
+                        ident[:],
+                        start=(d == 0),
+                        stop=(d == HOPS - 1),
+                        is_transpose=True,
                     )
+            if t % 2 == 1:
+                u = t // 2
+                for blk in range(TURNED // P):
+                    z_rows = keep.tile([P, P, 2], BF16, name="z_rows%d_%d" % (blk, u))
+                    nc.scalar.copy(z_rows[:], sums[blk][:, 2 * u : 2 * u + 2, :].rearrange("v e p -> v p e"))
+                    pairs = z_rows[:].rearrange("v p e -> v (p e)").bitcast(F32)
+                    nc.tensor.transpose(back_of[blk][:, u, :], pairs, ident[:])
+
+        late = []
+        for d in range(HOPS):
+            late.append(keep.tile([P, PACK, V - TURNED], F32, name="late%d" % d, tag="term%d_%d" % (PACK - 2, d)))
+        for t in range(PACK):
+            for d in range(HOPS):
+                gather_term(late[d][:, t, :], t, d, TURNED, V - TURNED)
+
+        g = keep.tile([P, V], F32, name="g")
+        for c, (v0, width) in enumerate(Z_GROUPS):
             z_bf = keep.tile([P, width, PACK], BF16, name="z_bf%d" % c, tag="z_bf%d" % (c % 2), align_bytes=64)
-            if c == len(V_CHUNKS) - 1:
+            if v0 == TURNED:
                 nc.vector.tensor_tensor(
                     z_bf[:].rearrange("p (c i) t -> p c t i", i=2),
-                    terms[0][:].rearrange("p t (c i) -> p c t i", i=2),
-                    terms[1][:].rearrange("p t (c i) -> p c t i", i=2),
+                    late[0][:].rearrange("p t (c i) -> p c t i", i=2),
+                    late[1][:].rearrange("p t (c i) -> p c t i", i=2),
                     ADD,
                 )
+                code_tag = "z_bf1"
             else:
-                blocks = width // P
-                sums = [psum.tile([P, PACK, P], F32, name="z_sum", tag="z_sum", bufs=2) for blk in range(blocks)]
-                for t in range(PACK):
-                    for blk in range(blocks):
-                        for d in range(2):
-                            nc.tensor.matmul(
-                                sums[blk][:, t, :],
-                                terms[d, t][:, blk * P : (blk + 1) * P],
-                                ident[:],
-                                start=(d == 0),
-                                stop=(d == 1),
-                                is_transpose=True,
-                            )
-                back = psum.tile([P, blocks, 2, P], F32, name="z_back", tag="z_back")
-                for blk in range(blocks):
-                    z_rows = keep.tile([P, 2, P, 2], BF16, name="z_rows%d_%d" % (c, blk))
-                    nc.scalar.copy(z_rows[:], sums[blk][:].rearrange("v (u e) p -> v u p e", e=2))
-                    pairs = z_rows[:].rearrange("v u p e -> v (u p e)").bitcast(F32)
-                    for u in range(2):
-                        nc.tensor.transpose(back[:, blk, u, :], pairs[:, u * P : (u + 1) * P], ident[:])
+                z_pairs = z_bf[:].rearrange("p v t -> p (v t)").bitcast(F32)
                 nc.scalar.copy(
-                    z_bf[:].rearrange("p v t -> p (v t)").bitcast(F32).rearrange("p (b v u) -> p b v u", b=blocks, u=2),
-                    back[:].rearrange("p b u v -> p b v u"),
+                    z_pairs.rearrange("p (b v u) -> p b v u", b=width // P, u=2),
+                    backs[c][:].rearrange("p b u v -> p b v u"),
                 )
-            z_code = keep.tile([P, width], U32, name="z_code%d" % c, tag="z_bf1" if c == 2 else "z_code%d" % c, align_bytes=64)
+                code_tag = "z_code%d" % c
+            z_code = keep.tile([P, width], U32, name="z_code%d" % c, tag=code_tag, align_bytes=64)
             z_scale = keep.tile([P, width], U8, name="z_scale%d" % c, align_bytes=64)
             nc.vector.quantize_mx(
                 out=z_code[:].bitcast(FP8X4), scales=z_scale[:], in_=z_bf[:].rearrange("p v t -> p (v t)")
             )
-            g_acc = psum.tile([P, width], F32, name="g_acc", tag="acc", bufs=5)
+            g_acc = bank_tile([P, width], "g_acc")
             nc.tensor.matmul_mx(
                 out=g_acc[:],
                 lhsT=w2_code[:].bitcast(FP8X4),
@@ -207,15 +222,19 @@ def tile_picked_hop2_relu_p_kernel(
             )
             nc.scalar.activation(g[:, v0 : v0 + width], g_acc[:], RELU)
 
+        first = keep.tile([P, U], F32, name="root_first")
+        nc.vector.tensor_tensor(first[:], g[:].indirect(nxt_sb[0][:]), gate2_sb[:, 0, :], MULT)
+        count = U // 2
+        second = []
         for a in range(2):
-            r0, count = a * U // 2, U // 2
-            last = []
-            for d in range(2):
-                term = keep.tile([P, count], F32, name="root_term%d_%d" % (a, d))
-                nc.vector.tensor_tensor(
-                    term[:], g[:].indirect(entries(nxt_sb[d], r0, count)), gate2_sb[:, d, r0 : r0 + count], MULT
-                )
-                last.append(term)
+            r0 = a * count
+            term = keep.tile([P, count], F32, name="root_second%d" % a)
+            nc.vector.tensor_tensor(
+                term[:], g[:].indirect(entries(nxt_sb[1], r0, count)), gate2_sb[:, 1, r0 : r0 + count], MULT
+            )
+            second.append(term)
+        for a in range(2):
+            r0 = a * count
             result = keep.tile([P, count], F32, name="result%d" % a)
-            nc.vector.tensor_tensor(result[:], last[0][:], last[1][:], ADD)
+            nc.vector.tensor_tensor(result[:], first[:, r0 : r0 + count], second[a][:], ADD)
             nc.sync.dma_start(out[:, r0 : r0 + count], result[:])

@@ -23,12 +23,14 @@ HOPS = 2
 STRIPE = 16
 QUADRANT = 32
 SCALE_STEP = 8
+RUN = 8
 BANK = 512
 BANKS = 8
 
 X_LEAD = 1024
-TURNED = 384
+TURNED = 256
 FIRST_PIECES = ((0, 256), (256, 256), (512, 256), (768, 128), (896, 128))
+H_BANKS = ((1, 2, 3, 4, 5), (6, 7), (0, 1), (2, 3))
 Z_GROUPS = ((0, 256), (256, 128), (TURNED, V - TURNED))
 
 
@@ -41,11 +43,8 @@ def tile_picked_hop2_relu_p_kernel(
         keep = ctx.enter_context(tc.tile_pool(name="keep", bufs=1))
         psum = ctx.enter_context(tc.psum_pool(name="psum", bufs=1))
 
-        taken = []
-
-        def bank_tile(shape, name):
-            taken.append(name)
-            return psum.tile(shape, F32, name=name, tag="bank%d" % (len(taken) % BANKS))
+        def bank_tile(shape, name, bank):
+            return psum.tile(shape, F32, name=name, tag="bank%d" % bank)
 
         def load_list(name, dram, count):
             tile = lists.tile([P, count // STRIPE], U16, name=name)
@@ -80,11 +79,16 @@ def tile_picked_hop2_relu_p_kernel(
                 x_scale[r:P:QUADRANT, :].bitcast(I32), picked_scale[SCALE_STEP * r : P : QUADRANT, :].bitcast(I32)
             )
 
-        gate_sb = keep.tile([P, HOPS, V], F32, name="gate_sb")
-        nc.sync.dma_start(gate_sb[:], gate.rearrange("d p v -> p d v"))
-        pos_sb = [load_list("pos1_sb", pos1, V), load_list("pos2_sb", pos2, V)]
+        gate_sb, pos_sb = [], []
+        for d, pos in enumerate((pos1, pos2)):
+            tile = keep.tile([P, V], F32, name="gate%d" % d, tag="gate%d" % d, align_bytes=64)
+            nc.sync.dma_start(tile[:], gate[d])
+            gate_sb.append(tile)
+            pos_sb.append(load_list("pos%d_sb" % (d + 1), pos, V))
         w2_raw = keep.tile([P, PACK, N], F32, name="w2_raw")
-        nc.sync.dma_start(w2_raw[:], w2.rearrange("(p j) n -> p j n", j=PACK))
+        w2_rows = w2.rearrange("(b t r) n -> t b r n", t=PACK, r=RUN)
+        for t in range(PACK):
+            nc.sync.dma_start(w2_raw[:, t, :], w2_rows[t])
         nxt_sb = [load_list("nxt1_sb", nxt1, U), load_list("nxt2_sb", nxt2, U)]
         gate2_sb = keep.tile([P, HOPS, U], F32, name="gate2_sb")
         nc.sync.dma_start(gate2_sb[:], gate2.rearrange("d p u -> p d u"))
@@ -95,36 +99,46 @@ def tile_picked_hop2_relu_p_kernel(
         x_code = keep.tile([P, S], U32, name="x_code", tag="in_turn", align_bytes=64)
         nc.vector.tensor_copy(x_code[:], word_table[:].indirect(offs_sb[:]))
 
-        w1_bf = keep.tile([P, PACK, P, PACK], BF16, name="w1_bf", align_bytes=64)
+        w1_bf = []
+        w1_bf2 = keep.tile([P, 2, P, PACK], BF16, name="w1_bf2", align_bytes=64)
 
-        def deal_w1(engine_copy, a, t0, t1):
-            src = w1_raw[a][:].rearrange("p j (m t) -> p m t j", t=PACK)[:, :, t0:t1, :]
-            dst = w1_bf[:].rearrange("p t m j -> p m t j")[:, a * P // 2 : (a + 1) * P // 2, t0:t1, :]
-            engine_copy(dst, src)
+        def deal_first(copy, a):
+            w1_bf.append(keep.tile([P, P, PACK], BF16, name="w1_bf%d" % a, tag="w1_bf", align_bytes=64))
+            src = w1_raw[a][:].rearrange("p j (b s c i) -> p s b c j i", s=2, c=RUN, i=2)[:, 0]
+            copy(w1_bf[a][:].rearrange("p (b c i) j -> p b c j i", c=RUN, i=2), src)
 
-        deal_w1(nc.scalar.copy, 0, 0, PACK)
-        deal_w1(nc.vector.tensor_copy, 1, 0, PACK // 2)
-        deal_w1(nc.scalar.copy, 1, PACK // 2, PACK)
-        w1_code, w1_scale = [], []
-        for t in range(PACK):
-            code = keep.tile([P, P], U32, name="w1_code%d" % t, align_bytes=64)
-            scale = keep.tile([P, P], U8, name="w1_scale%d" % t, align_bytes=64)
-            nc.vector.quantize_mx(
-                out=code[:].bitcast(FP8X4), scales=scale[:], in_=w1_bf[:, t, :, :].rearrange("p m j -> p (m j)")
-            )
-            w1_code.append(code)
-            w1_scale.append(scale)
+        def deal_second(copy, a, t):
+            src = w1_raw[a][:].rearrange("p j (b t c i) -> p t b c j i", t=PACK, c=RUN // 2, i=2)[:, t]
+            dst = w1_bf2[:, t - 2, a * P // 2 : (a + 1) * P // 2, :]
+            copy(dst.rearrange("p (b c i) j -> p b c j i", c=RUN // 2, i=2), src)
+
+        def quantise_w1(name, values, width):
+            code = keep.tile([P, width], U32, name=name + "_code", align_bytes=64)
+            scale = keep.tile([P, width], U8, name=name + "_scale", align_bytes=64)
+            nc.vector.quantize_mx(out=code[:].bitcast(FP8X4), scales=scale[:], in_=values)
+            return code, scale
+
+        deal_first(nc.scalar.copy, 0)
+        w1_q = [quantise_w1("w1_0", w1_bf[0][:].rearrange("p m j -> p (m j)"), P)]
+        deal_first(nc.vector.tensor_copy, 1)
+        for a in range(2):
+            for t in range(2, PACK):
+                deal_second(nc.scalar.copy, a, t)
+        w1_q.append(quantise_w1("w1_1", w1_bf[1][:].rearrange("p m j -> p (m j)"), P))
+        w1_q.append(quantise_w1("w1_2", w1_bf2[:].rearrange("p t m j -> p (t m j)"), 2 * P))
+        w1_code = [w1_q[0][0][:], w1_q[1][0][:], w1_q[2][0][:, :P], w1_q[2][0][:, P:]]
+        w1_scale = [w1_q[0][1][:], w1_q[1][1][:], w1_q[2][1][:, :P], w1_q[2][1][:, P:]]
 
         h = []
         for t in range(PACK):
-            h_t = keep.tile([P, S], F32, name="h%d" % t)
+            h_t = keep.tile([P, S], F32, name="h%d" % t, tag="h%d" % t, align_bytes=64)
             pieces = FIRST_PIECES if t == 0 else ((0, BANK), (BANK, BANK))
             for n, (s0, count) in enumerate(pieces):
-                acc = bank_tile([P, count], "h_acc")
+                acc = bank_tile([P, count], "h_acc", H_BANKS[t][n])
                 nc.tensor.matmul_mx(
                     out=acc[:],
-                    lhsT=w1_code[t][:].bitcast(FP8X4),
-                    lhsT_scale=w1_scale[t][:],
+                    lhsT=w1_code[t].bitcast(FP8X4),
+                    lhsT_scale=w1_scale[t],
                     rhs=x_code[:, s0 : s0 + count].bitcast(FP8X4),
                     rhs_scale=x_scale[:, s0 : s0 + count],
                     start=True,
@@ -142,31 +156,26 @@ def tile_picked_hop2_relu_p_kernel(
             w2_bf[:].rearrange("p (c i) j -> p c j i", i=2),
             w2_raw[:].rearrange("p j (c i) -> p c j i", i=2),
         )
-        w2_code = keep.tile([P, N], U32, name="w2_code", align_bytes=64)
-        w2_scale = keep.tile([P, N], U8, name="w2_scale", align_bytes=64)
-        nc.vector.quantize_mx(
-            out=w2_code[:].bitcast(FP8X4), scales=w2_scale[:], in_=w2_bf[:].rearrange("p n j -> p (n j)")
-        )
 
         def gather_term(dst, t, d, v0, width):
             nc.vector.tensor_tensor(
-                dst, h[t][:].indirect(entries(pos_sb[d], v0, width)), gate_sb[:, d, v0 : v0 + width], MULT
+                dst, h[t][:].indirect(entries(pos_sb[d], v0, width)), gate_sb[d][:, v0 : v0 + width], MULT
             )
 
-        sums = [bank_tile([P, PACK, P], "z_sum") for blk in range(TURNED // P)]
-        backs = [bank_tile([P, width // P, 2, P], "z_back") for v0, width in Z_GROUPS[:-1]]
-        back_of = [backs[c][:, b, :, :] for c, (v0, width) in enumerate(Z_GROUPS[:-1]) for b in range(width // P)]
+        blocks = V // P
+        early_blocks = TURNED // P
+        sums = [bank_tile([P, PACK, P], "z_sum", blk) for blk in range(blocks)]
+        early_back = bank_tile([P, early_blocks, 2, P], "z_back", 4)
+        late_back = bank_tile([P, blocks - early_blocks, P], "z_back_late", 5)
         for t in range(PACK):
-            early = []
+            width = V if t < 2 else TURNED
             for d in range(HOPS):
-                term = keep.tile([P, TURNED], F32, name="early%d_%d" % (t, d), tag="term%d_%d" % (t, d))
-                gather_term(term[:], t, d, 0, TURNED)
-                early.append(term)
-            for blk in range(TURNED // P):
-                for d in range(HOPS):
+                term = keep.tile([P, width], F32, name="early%d_%d" % (t, d), tag="term%d_%d" % (t, d), align_bytes=64)
+                gather_term(term[:], t, d, 0, width)
+                for blk in range(width // P):
                     nc.tensor.matmul(
                         sums[blk][:, t, :],
-                        early[d][:, blk * P : (blk + 1) * P],
+                        term[:, blk * P : (blk + 1) * P],
                         ident[:],
                         start=(d == 0),
                         stop=(d == HOPS - 1),
@@ -174,53 +183,80 @@ def tile_picked_hop2_relu_p_kernel(
                     )
             if t % 2 == 1:
                 u = t // 2
-                for blk in range(TURNED // P):
+                for blk in range(width // P):
                     z_rows = keep.tile([P, P, 2], BF16, name="z_rows%d_%d" % (blk, u))
-                    nc.scalar.copy(z_rows[:], sums[blk][:, 2 * u : 2 * u + 2, :].rearrange("v e p -> v p e"))
+                    if u == 0:
+                        nc.scalar.copy(
+                            z_rows[:].rearrange("v (b r) e -> v b r e", r=RUN),
+                            sums[blk][:, :2, :].rearrange("v a (b e r) -> v (a b) r e", e=2, r=RUN),
+                        )
+                    else:
+                        nc.scalar.copy(z_rows[:], sums[blk][:, 2:, :].rearrange("v e p -> v p e"))
                     pairs = z_rows[:].rearrange("v p e -> v (p e)").bitcast(F32)
-                    nc.tensor.transpose(back_of[blk][:, u, :], pairs, ident[:])
+                    back = early_back[:, blk, u, :] if blk < early_blocks else late_back[:, blk - early_blocks, :]
+                    nc.tensor.transpose(back, pairs, ident[:])
+            if t == 1:
+                z_late = []
+                for b in range(blocks - early_blocks):
+                    tile = keep.tile([P, P * PACK], BF16, name="z_late%d" % b, align_bytes=64)
+                    nc.scalar.copy(
+                        tile[:].bitcast(F32).rearrange("p (v u) -> p v u", u=2)[:, :, 0], late_back[:, b, :]
+                    )
+                    z_late.append(tile)
 
-        late = []
-        for d in range(HOPS):
-            late.append(keep.tile([P, PACK, V - TURNED], F32, name="late%d" % d, tag="term%d_%d" % (PACK - 2, d)))
-        for t in range(PACK):
+        late = [keep.tile([P, 2, V - TURNED], F32, name="late%d" % d, tag="term2_%d" % d, align_bytes=64) for d in range(HOPS)]
+        for t in range(2, PACK):
             for d in range(HOPS):
-                gather_term(late[d][:, t, :], t, d, TURNED, V - TURNED)
+                gather_term(late[d][:, t - 2, :], t, d, TURNED, V - TURNED)
+
+        w2_code = keep.tile([P, N], U32, name="w2_code", tag="gate0", align_bytes=64)
+        w2_scale = keep.tile([P, N], U8, name="w2_scale", align_bytes=64)
+        nc.vector.quantize_mx(
+            out=w2_code[:].bitcast(FP8X4), scales=w2_scale[:], in_=w2_bf[:].rearrange("p n j -> p (n j)")
+        )
+
+        def add_late(b):
+            cols = slice(b * P, (b + 1) * P)
+            nc.vector.tensor_tensor(
+                z_late[b][:].rearrange("p (c i u e) -> p c u e i", i=2, u=2, e=2)[:, :, 1],
+                late[0][:, :, cols].rearrange("p e (c i) -> p c e i", i=2),
+                late[1][:, :, cols].rearrange("p e (c i) -> p c e i", i=2),
+                ADD,
+            )
 
         g = keep.tile([P, V], F32, name="g")
-        for c, (v0, width) in enumerate(Z_GROUPS):
-            z_bf = keep.tile([P, width, PACK], BF16, name="z_bf%d" % c, tag="z_bf%d" % (c % 2), align_bytes=64)
-            if v0 == TURNED:
-                nc.vector.tensor_tensor(
-                    z_bf[:].rearrange("p (c i) t -> p c t i", i=2),
-                    late[0][:].rearrange("p t (c i) -> p c t i", i=2),
-                    late[1][:].rearrange("p t (c i) -> p c t i", i=2),
-                    ADD,
-                )
-                code_tag = "z_bf1"
-            else:
-                z_pairs = z_bf[:].rearrange("p v t -> p (v t)").bitcast(F32)
-                nc.scalar.copy(
-                    z_pairs.rearrange("p (b v u) -> p b v u", b=width // P, u=2),
-                    backs[c][:].rearrange("p b u v -> p b v u"),
-                )
-                code_tag = "z_code%d" % c
-            z_code = keep.tile([P, width], U32, name="z_code%d" % c, tag=code_tag, align_bytes=64)
+
+        def second_product(c, z_bf, z_code, v0, width, on_vector):
             z_scale = keep.tile([P, width], U8, name="z_scale%d" % c, align_bytes=64)
-            nc.vector.quantize_mx(
-                out=z_code[:].bitcast(FP8X4), scales=z_scale[:], in_=z_bf[:].rearrange("p v t -> p (v t)")
-            )
-            g_acc = bank_tile([P, width], "g_acc")
+            nc.vector.quantize_mx(out=z_code.bitcast(FP8X4), scales=z_scale[:], in_=z_bf[:])
+            g_acc = bank_tile([P, width], "g_acc", (6, 7, 0)[c])
             nc.tensor.matmul_mx(
                 out=g_acc[:],
                 lhsT=w2_code[:].bitcast(FP8X4),
                 lhsT_scale=w2_scale[:],
-                rhs=z_code[:].bitcast(FP8X4),
+                rhs=z_code.bitcast(FP8X4),
                 rhs_scale=z_scale[:],
                 start=True,
                 stop=True,
             )
-            nc.scalar.activation(g[:, v0 : v0 + width], g_acc[:], RELU)
+            cols = g[:, v0 : v0 + width]
+            if on_vector:
+                nc.vector.tensor_scalar_max(cols, g_acc[:], 0.0)
+            else:
+                nc.scalar.activation(cols, g_acc[:], RELU)
+
+        add_late(0)
+        z_early = keep.tile([P, TURNED * PACK], BF16, name="z_early", tag="z_early", align_bytes=64)
+        nc.scalar.copy(
+            z_early[:].bitcast(F32).rearrange("p (b v u) -> p b v u", b=early_blocks, u=2),
+            early_back[:].rearrange("p b u v -> p b v u"),
+        )
+        early_code = keep.tile([P, TURNED], U32, name="early_code", align_bytes=64)
+        second_product(0, z_early, early_code[:], 0, TURNED, False)
+        add_late(1)
+        late_code = keep.tile([P, V - TURNED], U32, name="late_code", tag="z_early", align_bytes=64)
+        second_product(1, z_late[0], late_code[:, :P], TURNED, P, False)
+        second_product(2, z_late[1], late_code[:, P:], TURNED + P, P, True)
 
         first = keep.tile([P, U], F32, name="root_first")
         nc.vector.tensor_tensor(first[:], g[:].indirect(nxt_sb[0][:]), gate2_sb[:, 0, :], MULT)

@@ -28,7 +28,7 @@ BANK = 512
 BANKS = 8
 
 X_LEAD = 1024
-TURNED = 256
+TURNED = 384
 FIRST_PIECES = ((0, 256), (256, 256), (512, 256), (768, 128), (896, 128))
 H_BANKS = ((1, 2, 3, 4, 5), (6, 7), (0, 1), (2, 3))
 Z_GROUPS = ((0, 256), (256, 128), (TURNED, V - TURNED))
@@ -85,7 +85,7 @@ def tile_picked_hop2_relu_p_kernel(
             nc.sync.dma_start(tile[:], gate[d])
             gate_sb.append(tile)
             pos_sb.append(load_list("pos%d_sb" % (d + 1), pos, V))
-        w2_raw = keep.tile([P, PACK, N], F32, name="w2_raw")
+        w2_raw = keep.tile([P, PACK, N], F32, name="w2_raw", tag="w2_raw", align_bytes=64)
         w2_rows = w2.rearrange("(b t r) n -> t b r n", t=PACK, r=RUN)
         for t in range(PACK):
             nc.sync.dma_start(w2_raw[:, t, :], w2_rows[t])
@@ -165,13 +165,15 @@ def tile_picked_hop2_relu_p_kernel(
         blocks = V // P
         early_blocks = TURNED // P
         sums = [bank_tile([P, PACK, P], "z_sum", blk) for blk in range(blocks)]
-        early_back = bank_tile([P, early_blocks, 2, P], "z_back", 4)
-        late_back = bank_tile([P, blocks - early_blocks, P], "z_back_late", 5)
+        early_back = [bank_tile([P, 2, P], "z_back", bank) for bank in (4, 5, 6)]
+        late_back = bank_tile([P, blocks - early_blocks, P], "z_back_late", 7)
         for t in range(PACK):
             width = V if t < 2 else TURNED
             for d in range(HOPS):
                 term = keep.tile([P, width], F32, name="early%d_%d" % (t, d), tag="term%d_%d" % (t, d), align_bytes=64)
-                gather_term(term[:], t, d, 0, width)
+                cuts = (0, 2 * P, width) if (t, d) == (PACK - 1, HOPS - 1) else (0, width)
+                for v0, v1 in zip(cuts, cuts[1:]):
+                    gather_term(term[:, v0:v1], t, d, v0, v1 - v0)
                 for blk in range(width // P):
                     nc.tensor.matmul(
                         sums[blk][:, t, :],
@@ -184,7 +186,7 @@ def tile_picked_hop2_relu_p_kernel(
             if t % 2 == 1:
                 u = t // 2
                 for blk in range(width // P):
-                    z_rows = keep.tile([P, P, 2], BF16, name="z_rows%d_%d" % (blk, u))
+                    z_rows = keep.tile([P, P, 2], BF16, name="z_rows", tag="z_rows%d_%d" % (blk, u), align_bytes=64)
                     if u == 0:
                         nc.scalar.copy(
                             z_rows[:].rearrange("v (b r) e -> v b r e", r=RUN),
@@ -193,7 +195,7 @@ def tile_picked_hop2_relu_p_kernel(
                     else:
                         nc.scalar.copy(z_rows[:], sums[blk][:, 2:, :].rearrange("v e p -> v p e"))
                     pairs = z_rows[:].rearrange("v p e -> v (p e)").bitcast(F32)
-                    back = early_back[:, blk, u, :] if blk < early_blocks else late_back[:, blk - early_blocks, :]
+                    back = early_back[blk][:, u, :] if blk < early_blocks else late_back[:, blk - early_blocks, :]
                     nc.tensor.transpose(back, pairs, ident[:])
             if t == 1:
                 z_late = []
@@ -204,10 +206,10 @@ def tile_picked_hop2_relu_p_kernel(
                     )
                     z_late.append(tile)
 
-        late = [keep.tile([P, 2, V - TURNED], F32, name="late%d" % d, tag="term2_%d" % d, align_bytes=64) for d in range(HOPS)]
+        late = keep.tile([P, HOPS, 2, V - TURNED], F32, name="late", tag="w2_raw", align_bytes=64)
         for t in range(2, PACK):
             for d in range(HOPS):
-                gather_term(late[d][:, t - 2, :], t, d, TURNED, V - TURNED)
+                gather_term(late[:, d, t - 2, :], t, d, TURNED, V - TURNED)
 
         w2_code = keep.tile([P, N], U32, name="w2_code", tag="gate0", align_bytes=64)
         w2_scale = keep.tile([P, N], U8, name="w2_scale", align_bytes=64)
@@ -219,44 +221,47 @@ def tile_picked_hop2_relu_p_kernel(
             cols = slice(b * P, (b + 1) * P)
             nc.vector.tensor_tensor(
                 z_late[b][:].rearrange("p (c i u e) -> p c u e i", i=2, u=2, e=2)[:, :, 1],
-                late[0][:, :, cols].rearrange("p e (c i) -> p c e i", i=2),
-                late[1][:, :, cols].rearrange("p e (c i) -> p c e i", i=2),
+                late[:, 0, :, cols].rearrange("p e (c i) -> p c e i", i=2),
+                late[:, 1, :, cols].rearrange("p e (c i) -> p c e i", i=2),
                 ADD,
             )
 
         g = keep.tile([P, V], F32, name="g")
 
-        def second_product(c, z_bf, z_code, v0, width, on_vector):
-            z_scale = keep.tile([P, width], U8, name="z_scale%d" % c, align_bytes=64)
-            nc.vector.quantize_mx(out=z_code.bitcast(FP8X4), scales=z_scale[:], in_=z_bf[:])
-            g_acc = bank_tile([P, width], "g_acc", (6, 7, 0)[c])
+        def second_product(blk, z_bf, bank, on_vector):
+            tag = "z_rows2_1" if blk == early_blocks else "z_code%d" % blk
+            z_code = keep.tile([P, P], U32, name="z_code", tag=tag, align_bytes=64)
+            z_scale = keep.tile([P, P], U8, name="z_scale%d" % blk, align_bytes=64)
+            nc.vector.quantize_mx(out=z_code[:].bitcast(FP8X4), scales=z_scale[:], in_=z_bf[:])
+            g_acc = bank_tile([P, P], "g_acc", bank)
             nc.tensor.matmul_mx(
                 out=g_acc[:],
                 lhsT=w2_code[:].bitcast(FP8X4),
                 lhsT_scale=w2_scale[:],
-                rhs=z_code.bitcast(FP8X4),
+                rhs=z_code[:].bitcast(FP8X4),
                 rhs_scale=z_scale[:],
                 start=True,
                 stop=True,
             )
-            cols = g[:, v0 : v0 + width]
+            cols = g[:, blk * P : (blk + 1) * P]
             if on_vector:
                 nc.vector.tensor_scalar_max(cols, g_acc[:], 0.0)
             else:
                 nc.scalar.activation(cols, g_acc[:], RELU)
 
         add_late(0)
-        z_early = keep.tile([P, TURNED * PACK], BF16, name="z_early", tag="z_early", align_bytes=64)
-        nc.scalar.copy(
-            z_early[:].bitcast(F32).rearrange("p (b v u) -> p b v u", b=early_blocks, u=2),
-            early_back[:].rearrange("p b u v -> p b v u"),
-        )
-        early_code = keep.tile([P, TURNED], U32, name="early_code", align_bytes=64)
-        second_product(0, z_early, early_code[:], 0, TURNED, False)
-        add_late(1)
-        late_code = keep.tile([P, V - TURNED], U32, name="late_code", tag="z_early", align_bytes=64)
-        second_product(1, z_late[0], late_code[:, :P], TURNED, P, False)
-        second_product(2, z_late[1], late_code[:, P:], TURNED + P, P, True)
+        z_early = []
+        for blk in range(early_blocks):
+            tile = keep.tile([P, P * PACK], BF16, name="z_early%d" % blk, align_bytes=64)
+            nc.scalar.copy(
+                tile[:].bitcast(F32).rearrange("p (v u) -> p v u", u=2),
+                early_back[blk][:].rearrange("p u v -> p v u"),
+            )
+            z_early.append(tile)
+        second_product(0, z_early[0], 5, False)
+        second_product(3, z_late[0], 6, False)
+        second_product(1, z_early[1], 4, False)
+        second_product(2, z_early[2], 0, True)
 
         first = keep.tile([P, U], F32, name="root_first")
         nc.vector.tensor_tensor(first[:], g[:].indirect(nxt_sb[0][:]), gate2_sb[:, 0, :], MULT)

@@ -16,6 +16,7 @@ FP8X4 = mybir.dt.float8_e4m3fn_x4
 MULT = mybir.AluOpType.mult
 ADD = mybir.AluOpType.add
 RELU = mybir.ActivationFunctionType.Relu
+COPY = mybir.ActivationFunctionType.Copy
 
 P = 128
 PACK = 4
@@ -23,15 +24,14 @@ HOPS = 2
 STRIPE = 16
 QUADRANT = 32
 SCALE_STEP = 8
-RUN = 8
 BANK = 512
-BANKS = 8
 
-X_LEAD = 1024
-TURNED = 384
-FIRST_PIECES = ((0, 256), (256, 256), (512, 256), (768, 128), (896, 128))
-H_BANKS = ((1, 2, 3, 4, 5), (6, 7), (0, 1), (2, 3))
-Z_GROUPS = ((0, 256), (256, 128), (TURNED, V - TURNED))
+X_LEAD = 768
+X_FIRST = 768
+FIRST_PIECES = ((0, 256), (256, 256), (512, 256), (768, 256))
+H_BANKS = ((0, 1, 2, 3), (4, 5, 6, 7), (0, 1), (2, 3))
+TURNED = 256
+FETCHED = 256
 
 
 def tile_picked_hop2_relu_p_kernel(
@@ -58,8 +58,9 @@ def tile_picked_hop2_relu_p_kernel(
         word_rows = x_words[0].rearrange("p n t -> p (n t)").bitcast(I32)
         nc.sync.dma_start(word_table[:, :X_LEAD].bitcast(I32), word_rows[:, :X_LEAD])
         offs_sb = load_list("offs_sb", offs, S)
+        pos_sb = [load_list("pos1_sb", pos1, V)]
 
-        scale_table = keep.tile([P, T], U8, name="scale_table", tag="in_turn", align_bytes=64)
+        scale_table = keep.tile([P, T], U8, name="scale_table", tag="scale_table", align_bytes=64)
         nc.vector.memset(scale_table[:].bitcast(I32), 0)
         nc.sync.dma_start(scale_table[0:P:SCALE_STEP, :].bitcast(I32), x_scales[0].bitcast(I32))
         nc.sync.dma_start(word_table[:, X_LEAD:].bitcast(I32), word_rows[:, X_LEAD:])
@@ -68,169 +69,211 @@ def tile_picked_hop2_relu_p_kernel(
         half = H // 2
         w1_raw = [keep.tile([P, PACK, half], F32, name="w1_raw%d" % a) for a in range(2)]
         nc.sync.dma_start(w1_raw[0][:], w1_rows[:, :, :half])
-        nc.sync.dma_start(w1_raw[1][:], w1_rows[:, :, half:])
+        pos_sb.append(load_list("pos2_sb", pos2, V))
 
         x_scale = keep.tile([P, S], U8, name="x_scale", align_bytes=64)
         nc.vector.memset(x_scale[:].bitcast(I32), 0)
-        picked_scale = keep.tile([P, S], U8, name="picked_scale", align_bytes=64)
+        picked_scale = keep.tile([P, S], U8, name="picked_scale", tag="picked", align_bytes=64)
         nc.vector.tensor_copy(picked_scale[:], scale_table[:].indirect(offs_sb[:]))
         for r in range(QUADRANT // SCALE_STEP):
             nc.sync.dma_start(
                 x_scale[r:P:QUADRANT, :].bitcast(I32), picked_scale[SCALE_STEP * r : P : QUADRANT, :].bitcast(I32)
             )
 
-        gate_sb, pos_sb = [], []
-        for d, pos in enumerate((pos1, pos2)):
-            tile = keep.tile([P, V], F32, name="gate%d" % d, tag="gate%d" % d, align_bytes=64)
+        nc.sync.dma_start(w1_raw[1][:], w1_rows[:, :, half:])
+        w2_raw = keep.tile([P, PACK, N], F32, name="w2_raw", align_bytes=64)
+        nc.sync.dma_start(w2_raw[:], w2.rearrange("(p j) n -> p j n", j=PACK))
+        gate_sb = []
+        for d in range(HOPS):
+            tile = keep.tile([P, V], F32, name="gate%d" % d, align_bytes=64)
             nc.sync.dma_start(tile[:], gate[d])
             gate_sb.append(tile)
-            pos_sb.append(load_list("pos%d_sb" % (d + 1), pos, V))
-        w2_raw = keep.tile([P, PACK, N], F32, name="w2_raw", tag="w2_raw", align_bytes=64)
-        w2_rows = w2.rearrange("(b t r) n -> t b r n", t=PACK, r=RUN)
-        for t in range(PACK):
-            nc.sync.dma_start(w2_raw[:, t, :], w2_rows[t])
+        gate_col = keep.tile([P, HOPS, 8], F32, name="gate_col")
+        with nc.allow_non_contiguous_dma(reason="one weight a partition"):
+            for d in range(HOPS):
+                nc.sync.dma_start(gate_col[:, d, : FETCHED // P], gate[d, 0, :FETCHED].rearrange("(b v) -> v b", v=P))
         nxt_sb = [load_list("nxt1_sb", nxt1, U), load_list("nxt2_sb", nxt2, U)]
         gate2_sb = keep.tile([P, HOPS, U], F32, name="gate2_sb")
         nc.sync.dma_start(gate2_sb[:], gate2.rearrange("d p u -> p d u"))
 
-        ident = keep.tile([P, P], F32, name="ident")
+        ident = keep.tile([P, P], F32, name="ident", tag="scale_table", align_bytes=64)
         make_identity(nc, ident[:])
 
-        x_code = keep.tile([P, S], U32, name="x_code", tag="in_turn", align_bytes=64)
-        nc.vector.tensor_copy(x_code[:], word_table[:].indirect(offs_sb[:]))
+        x_first = keep.tile([P, X_FIRST], U32, name="x_first", align_bytes=64)
+        nc.vector.tensor_copy(x_first[:], word_table[:].indirect(entries(offs_sb, 0, X_FIRST)))
 
         w1_bf = []
         w1_bf2 = keep.tile([P, 2, P, PACK], BF16, name="w1_bf2", align_bytes=64)
 
         def deal_first(copy, a):
-            w1_bf.append(keep.tile([P, P, PACK], BF16, name="w1_bf%d" % a, tag="w1_bf", align_bytes=64))
-            src = w1_raw[a][:].rearrange("p j (b s c i) -> p s b c j i", s=2, c=RUN, i=2)[:, 0]
-            copy(w1_bf[a][:].rearrange("p (b c i) j -> p b c j i", c=RUN, i=2), src)
+            w1_bf.append(keep.tile([P, P, PACK], BF16, name="w1_bf%d" % a, align_bytes=64))
+            src = w1_raw[a][:].rearrange("p j (q u e) -> p u q j e", u=2, e=2)[:, 0]
+            copy(w1_bf[a][:].rearrange("p (q e) j -> p q j e", e=2), src)
 
-        def deal_second(copy, a, t):
-            src = w1_raw[a][:].rearrange("p j (b t c i) -> p t b c j i", t=PACK, c=RUN // 2, i=2)[:, t]
-            dst = w1_bf2[:, t - 2, a * P // 2 : (a + 1) * P // 2, :]
-            copy(dst.rearrange("p (b c i) j -> p b c j i", c=RUN // 2, i=2), src)
+        def deal_second(copy, a):
+            src = w1_raw[a][:].rearrange("p j (c i u e) -> p u c j i e", i=2, u=2, e=2)[:, 1]
+            dst = w1_bf2[:, :, a * P // 2 : (a + 1) * P // 2, :]
+            copy(dst.rearrange("p e (c i) j -> p c j i e", i=2), src)
 
         def quantise_w1(name, values, width):
-            code = keep.tile([P, width], U32, name=name + "_code", align_bytes=64)
-            scale = keep.tile([P, width], U8, name=name + "_scale", align_bytes=64)
+            code = keep.tile([P, width], U32, name=name + "_code", tag=name + "_code", align_bytes=64)
+            scale = keep.tile([P, width], U8, name=name + "_scale", tag=name + "_scale", align_bytes=64)
             nc.vector.quantize_mx(out=code[:].bitcast(FP8X4), scales=scale[:], in_=values)
             return code, scale
 
         deal_first(nc.scalar.copy, 0)
         w1_q = [quantise_w1("w1_0", w1_bf[0][:].rearrange("p m j -> p (m j)"), P)]
+        x_last = keep.tile([P, S - X_FIRST], U32, name="x_last", tag="picked", align_bytes=64)
+        nc.vector.tensor_copy(x_last[:], word_table[:].indirect(entries(offs_sb, X_FIRST, S - X_FIRST)))
+        deal_second(nc.scalar.copy, 0)
         deal_first(nc.vector.tensor_copy, 1)
-        for a in range(2):
-            for t in range(2, PACK):
-                deal_second(nc.scalar.copy, a, t)
+        deal_second(nc.vector.tensor_copy, 1)
         w1_q.append(quantise_w1("w1_1", w1_bf[1][:].rearrange("p m j -> p (m j)"), P))
+        w2_bf = keep.tile([P, N, PACK], BF16, name="w2_bf", align_bytes=64)
+        nc.vector.tensor_copy(
+            w2_bf[:].rearrange("p (c i) j -> p c j i", i=2),
+            w2_raw[:].rearrange("p j (c i) -> p c j i", i=2),
+        )
         w1_q.append(quantise_w1("w1_2", w1_bf2[:].rearrange("p t m j -> p (t m j)"), 2 * P))
+        w2_code = keep.tile([P, N], U32, name="w2_code", align_bytes=64)
+        w2_scale = keep.tile([P, N], U8, name="w2_scale", align_bytes=64)
+        nc.vector.quantize_mx(
+            out=w2_code[:].bitcast(FP8X4), scales=w2_scale[:], in_=w2_bf[:].rearrange("p n j -> p (n j)")
+        )
         w1_code = [w1_q[0][0][:], w1_q[1][0][:], w1_q[2][0][:, :P], w1_q[2][0][:, P:]]
         w1_scale = [w1_q[0][1][:], w1_q[1][1][:], w1_q[2][1][:, :P], w1_q[2][1][:, P:]]
 
         h = []
-        for t in range(PACK):
+        fetched = {}
+
+        def fetch(t):
+            for d in range(HOPS):
+                tag = ("w1_1_code", "w1_1_scale")[d] if t == 0 else "fetched%d" % d
+                tile = keep.tile([P, FETCHED], F32, name="fetched%d_%d" % (t, d), tag=tag, align_bytes=64)
+                nc.scalar.activation(tile[:], h[t][:].indirect(entries(pos_sb[d], 0, FETCHED)), COPY)
+                fetched[t, d] = tile
+
+        def product(acc, t, s0, count):
+            codes = x_first[:, s0 : s0 + count] if s0 < X_FIRST else x_last[:, s0 - X_FIRST : s0 - X_FIRST + count]
+            nc.tensor.matmul_mx(
+                out=acc,
+                lhsT=w1_code[t].bitcast(FP8X4),
+                lhsT_scale=w1_scale[t],
+                rhs=codes.bitcast(FP8X4),
+                rhs_scale=x_scale[:, s0 : s0 + count],
+                start=True,
+                stop=True,
+            )
+
+        def make_h(t):
             h_t = keep.tile([P, S], F32, name="h%d" % t, tag="h%d" % t, align_bytes=64)
-            pieces = FIRST_PIECES if t == 0 else ((0, BANK), (BANK, BANK))
+            pieces = FIRST_PIECES if t < 2 else ((0, BANK), (BANK, BANK))
             for n, (s0, count) in enumerate(pieces):
                 acc = bank_tile([P, count], "h_acc", H_BANKS[t][n])
-                nc.tensor.matmul_mx(
-                    out=acc[:],
-                    lhsT=w1_code[t].bitcast(FP8X4),
-                    lhsT_scale=w1_scale[t],
-                    rhs=x_code[:, s0 : s0 + count].bitcast(FP8X4),
-                    rhs_scale=x_scale[:, s0 : s0 + count],
-                    start=True,
-                    stop=True,
-                )
-                cols = h_t[:, s0 : s0 + count]
-                if t == 0 and n % 2 == 1:
-                    nc.vector.tensor_scalar_max(cols, acc[:], 0.0)
-                else:
-                    nc.scalar.activation(cols, acc[:], RELU)
+                cuts = (s0, X_FIRST, s0 + count) if s0 < X_FIRST < s0 + count else (s0, s0 + count)
+                for c0, c1 in zip(cuts, cuts[1:]):
+                    product(acc[:, c0 - s0 : c1 - s0], t, c0, c1 - c0)
+                nc.scalar.activation(h_t[:, s0 : s0 + count], acc[:], RELU)
             h.append(h_t)
-
-        w2_bf = keep.tile([P, N, PACK], BF16, name="w2_bf", tag="in_turn", align_bytes=64)
-        nc.scalar.copy(
-            w2_bf[:].rearrange("p (c i) j -> p c j i", i=2),
-            w2_raw[:].rearrange("p j (c i) -> p c j i", i=2),
-        )
 
         def gather_term(dst, t, d, v0, width):
             nc.vector.tensor_tensor(
                 dst, h[t][:].indirect(entries(pos_sb[d], v0, width)), gate_sb[d][:, v0 : v0 + width], MULT
             )
 
-        blocks = V // P
-        early_blocks = TURNED // P
-        sums = [bank_tile([P, PACK, P], "z_sum", blk) for blk in range(blocks)]
-        early_back = [bank_tile([P, 2, P], "z_back", bank) for bank in (4, 5, 6)]
-        late_back = bank_tile([P, blocks - early_blocks, P], "z_back_late", 7)
-        for t in range(PACK):
-            width = V if t < 2 else TURNED
+        def pair_view(rows, u):
+            if u == 0:
+                return rows.rearrange("v a (q e) -> v (a q) e", e=2)
+            return rows.rearrange("v e p -> v p e")
+
+        def turn_terms(t, d, term, v0, blocks):
+            for blk in blocks:
+                nc.tensor.matmul(
+                    sums[blk][:, t % 2, :],
+                    term[:, blk * P - v0 : (blk + 1) * P - v0],
+                    ident[:],
+                    start=(d == 0),
+                    stop=(d == HOPS - 1),
+                    is_transpose=True,
+                )
+
+        def gather_first_pair(t):
             for d in range(HOPS):
-                term = keep.tile([P, width], F32, name="early%d_%d" % (t, d), tag="term%d_%d" % (t, d), align_bytes=64)
-                cuts = (0, 2 * P, width) if (t, d) == (PACK - 1, HOPS - 1) else (0, width)
-                for v0, v1 in zip(cuts, cuts[1:]):
-                    gather_term(term[:, v0:v1], t, d, v0, v1 - v0)
-                for blk in range(width // P):
-                    nc.tensor.matmul(
-                        sums[blk][:, t, :],
-                        term[:, blk * P : (blk + 1) * P],
-                        ident[:],
-                        start=(d == 0),
-                        stop=(d == HOPS - 1),
-                        is_transpose=True,
-                    )
-            if t % 2 == 1:
-                u = t // 2
-                for blk in range(width // P):
-                    z_rows = keep.tile([P, P, 2], BF16, name="z_rows", tag="z_rows%d_%d" % (blk, u), align_bytes=64)
-                    if u == 0:
-                        nc.scalar.copy(
-                            z_rows[:].rearrange("v (b r) e -> v b r e", r=RUN),
-                            sums[blk][:, :2, :].rearrange("v a (b e r) -> v (a b) r e", e=2, r=RUN),
-                        )
-                    else:
-                        nc.scalar.copy(z_rows[:], sums[blk][:, 2:, :].rearrange("v e p -> v p e"))
-                    pairs = z_rows[:].rearrange("v p e -> v (p e)").bitcast(F32)
-                    back = early_back[blk][:, u, :] if blk < early_blocks else late_back[:, blk - early_blocks, :]
-                    nc.tensor.transpose(back, pairs, ident[:])
-            if t == 1:
-                z_late = []
-                for b in range(blocks - early_blocks):
-                    tile = keep.tile([P, P * PACK], BF16, name="z_late%d" % b, align_bytes=64)
-                    nc.scalar.copy(
-                        tile[:].bitcast(F32).rearrange("p (v u) -> p v u", u=2)[:, :, 0], late_back[:, b, :]
-                    )
-                    z_late.append(tile)
+                term = keep.tile([P, V - FETCHED], F32, name="term%d_%d" % (t, d), align_bytes=64)
+                gather_term(term[:], t, d, FETCHED, V - FETCHED)
+                turn_terms(t, d, term, FETCHED, range(FETCHED // P, V // P))
 
-        late = keep.tile([P, HOPS, 2, V - TURNED], F32, name="late", tag="w2_raw", align_bytes=64)
-        for t in range(2, PACK):
+        def gather_second_pair(t, v0, v1):
             for d in range(HOPS):
-                gather_term(late[:, d, t - 2, :], t, d, TURNED, V - TURNED)
+                gather_term(second_terms[d][:, t - 2, v0:v1], t, d, v0, v1 - v0)
+                if v0 < TURNED:
+                    turn_terms(t, d, second_terms[d][:, t - 2, :], 0, range(TURNED // P))
 
-        w2_code = keep.tile([P, N], U32, name="w2_code", tag="gate0", align_bytes=64)
-        w2_scale = keep.tile([P, N], U8, name="w2_scale", align_bytes=64)
-        nc.vector.quantize_mx(
-            out=w2_code[:].bitcast(FP8X4), scales=w2_scale[:], in_=w2_bf[:].rearrange("p n j -> p (n j)")
-        )
+        def turn_plain(t):
+            for d in range(HOPS):
+                for blk in range(FETCHED // P):
+                    nc.tensor.transpose(plain[blk][:, d, t, :], fetched[t, d][:, blk * P : (blk + 1) * P], ident[:])
 
-        def add_late(b):
-            cols = slice(b * P, (b + 1) * P)
-            nc.vector.tensor_tensor(
-                z_late[b][:].rearrange("p (c i u e) -> p c u e i", i=2, u=2, e=2)[:, :, 1],
-                late[:, 0, :, cols].rearrange("p e (c i) -> p c e i", i=2),
-                late[:, 1, :, cols].rearrange("p e (c i) -> p c e i", i=2),
-                ADD,
+        z_rows = {}
+
+        def round_rows(blk, u):
+            rows = keep.tile([P, P, 2], BF16, name="z_rows%d_%d" % (blk, u), align_bytes=64)
+            nc.scalar.copy(rows[:], pair_view(sums[blk], u))
+            z_rows[blk, u] = rows
+
+        def scale_first(blk):
+            tile = keep.tile([P, P, 2], F32, name="scaled%d" % blk, align_bytes=64)
+            nc.scalar.activation(tile[:], pair_view(plain[blk][:, 0], 0), COPY, scale=gate_col[:, 0, blk : blk + 1])
+            return tile
+
+        def add_second(blk, scaled):
+            rows = keep.tile([P, P, 2], BF16, name="z_rows%d_0" % blk, align_bytes=64)
+            nc.vector.scalar_tensor_tensor(
+                rows[:], pair_view(plain[blk][:, 1], 0), gate_col[:, 1, blk : blk + 1], scaled[:], MULT, ADD
             )
+            z_rows[blk, 0] = rows
+
+        def turn_back(blk, u, back):
+            nc.tensor.transpose(back, z_rows[blk, u][:].rearrange("v p e -> v (p e)").bitcast(F32), ident[:])
+
+        make_h(0)
+        make_h(1)
+        make_h(2)
+        fetch(0)
+        make_h(3)
+        fetch(1)
+        plain = [bank_tile([P, HOPS, 2, P], "z_plain", bank) for bank in (4, 5)]
+        sums = [bank_tile([P, 2, P], "z_sum", bank)[:] for bank in (0, 1, 6, 7)]
+        second_terms = [keep.tile([P, 2, V], F32, name="second_terms%d" % d, align_bytes=64) for d in range(HOPS)]
+        gather_first_pair(0)
+        gather_first_pair(1)
+        turn_plain(0)
+        gather_second_pair(2, 0, V)
+        turn_plain(1)
+        gather_second_pair(3, 0, TURNED)
+        gather_second_pair(3, TURNED, V)
+        late_back = bank_tile([P, 2, P], "z_back_late", 2)
+        for blk in (2, 3):
+            round_rows(blk, 0)
+            turn_back(blk, 0, late_back[:, blk - 2, :])
+        scaled = [scale_first(blk) for blk in range(2)]
+        early_back = [bank_tile([P, 2, P], "z_back", bank) for bank in (3, 6)]
+        for blk in range(2):
+            round_rows(blk, 1)
+            turn_back(blk, 1, early_back[blk][:, 1, :])
+        for blk in range(2):
+            add_second(blk, scaled[blk])
+            turn_back(blk, 0, early_back[blk][:, 0, :])
+        z_late = []
+        for b in range(2):
+            tile = keep.tile([P, P * PACK], BF16, name="z_late%d" % b, align_bytes=64)
+            nc.scalar.copy(tile[:].bitcast(F32).rearrange("p (v u) -> p v u", u=2)[:, :, 0], late_back[:, b, :])
+            z_late.append(tile)
 
         g = keep.tile([P, V], F32, name="g")
 
         def second_product(blk, z_bf, bank, on_vector):
-            tag = "z_rows2_1" if blk == early_blocks else "z_code%d" % blk
-            z_code = keep.tile([P, P], U32, name="z_code", tag=tag, align_bytes=64)
+            z_code = keep.tile([P, P], U32, name="z_code%d" % blk, align_bytes=64)
             z_scale = keep.tile([P, P], U8, name="z_scale%d" % blk, align_bytes=64)
             nc.vector.quantize_mx(out=z_code[:].bitcast(FP8X4), scales=z_scale[:], in_=z_bf[:])
             g_acc = bank_tile([P, P], "g_acc", bank)
@@ -249,33 +292,38 @@ def tile_picked_hop2_relu_p_kernel(
             else:
                 nc.scalar.activation(cols, g_acc[:], RELU)
 
-        add_late(0)
+        for b in range(2):
+            cols = slice(TURNED + b * P, TURNED + (b + 1) * P)
+            nc.vector.tensor_tensor(
+                z_late[b][:].rearrange("p (c i u e) -> p c u e i", i=2, u=2, e=2)[:, :, 1],
+                second_terms[0][:, :, cols].rearrange("p e (c i) -> p c e i", i=2),
+                second_terms[1][:, :, cols].rearrange("p e (c i) -> p c e i", i=2),
+                ADD,
+            )
         z_early = []
-        for blk in range(early_blocks):
+        for blk in range(2):
             tile = keep.tile([P, P * PACK], BF16, name="z_early%d" % blk, align_bytes=64)
             nc.scalar.copy(
                 tile[:].bitcast(F32).rearrange("p (v u) -> p v u", u=2),
                 early_back[blk][:].rearrange("p u v -> p v u"),
             )
             z_early.append(tile)
-        second_product(0, z_early[0], 5, False)
-        second_product(3, z_late[0], 6, False)
-        second_product(1, z_early[1], 4, False)
-        second_product(2, z_early[2], 0, True)
+        second_product(2, z_late[0], 7, False)
+        second_product(3, z_late[1], 0, False)
+        second_product(0, z_early[0], 1, False)
+        second_product(1, z_early[1], 4, True)
 
+        count = U // 2
+        halves = [slice(a * count, (a + 1) * count) for a in range(2)]
+        second = keep.tile([P, U], F32, name="root_second")
+        for a in range(2):
+            nc.scalar.activation(second[:, halves[a]], g[:].indirect(entries(nxt_sb[1], a * count, count)), COPY)
         first = keep.tile([P, U], F32, name="root_first")
         nc.vector.tensor_tensor(first[:], g[:].indirect(nxt_sb[0][:]), gate2_sb[:, 0, :], MULT)
-        count = U // 2
-        second = []
-        for a in range(2):
-            r0 = a * count
-            term = keep.tile([P, count], F32, name="root_second%d" % a)
-            nc.vector.tensor_tensor(
-                term[:], g[:].indirect(entries(nxt_sb[1], r0, count)), gate2_sb[:, 1, r0 : r0 + count], MULT
-            )
-            second.append(term)
-        for a in range(2):
-            r0 = a * count
+        weighed = keep.tile([P, U], F32, name="root_weighed")
+        for cols in halves:
+            nc.vector.tensor_tensor(weighed[:, cols], second[:, cols], gate2_sb[:, 1, cols], MULT)
+        for a, cols in enumerate(halves):
             result = keep.tile([P, count], F32, name="result%d" % a)
-            nc.vector.tensor_tensor(result[:], first[:, r0 : r0 + count], second[a][:], ADD)
-            nc.sync.dma_start(out[:, r0 : r0 + count], result[:])
+            nc.vector.tensor_tensor(result[:], first[:, cols], weighed[:, cols], ADD)
+            nc.sync.dma_start(out[:, cols], result[:])

@@ -25,19 +25,26 @@ STRIPE = 16
 QUADRANT = 32
 SCALE_STEP = 8
 BANK = 512
+BLOCK_WORDS = 8
 
 X_LEAD = 768
 X_FIRST = 768
-FIRST_PIECES = ((0, 256), (256, 256), (512, 256), (768, 256))
+LOW = 256
+H_WIDTHS = (256, 256, BANK, BANK)
 H_BANKS = ((0, 1, 2, 3), (4, 5, 6, 7), (0, 1), (2, 3))
-TURNED = 256
-FETCHED = 256
+PLAIN_BANKS = (4, 5)
+SUM_BANKS = (0, 1, 6, 7)
+LOW_BACK_BANKS = (3, 6)
+HIGH_BACK_BANK = 2
+G_BANKS = (1, 4, 7, 0)
 
 
 def tile_picked_hop2_relu_p_kernel(
     tc, x_words, x_scales, w1, w2, gate, gate2, offs, pos1, pos2, nxt1, nxt2, out
 ):
     nc = tc.nc
+    low_groups = range(LOW // P)
+    high_groups = range(LOW // P, V // P)
     with ExitStack() as ctx:
         lists = ctx.enter_context(tc.tile_pool(name="lists", bufs=1))
         keep = ctx.enter_context(tc.tile_pool(name="keep", bufs=1))
@@ -53,6 +60,23 @@ def tile_picked_hop2_relu_p_kernel(
 
         def entries(tile, start, count):
             return tile[:, start // STRIPE : (start + count) // STRIPE]
+
+        def quantise(name, values, width):
+            code = keep.tile([P, width], U32, name=name + "_code", tag=name + "_code", align_bytes=64)
+            scale = keep.tile([P, width], U8, name=name + "_scale", tag=name + "_scale", align_bytes=64)
+            nc.vector.quantize_mx(out=code[:].bitcast(FP8X4), scales=scale[:], in_=values)
+            return code, scale
+
+        def product(acc, weight_code, weight_scale, moving_code, moving_scale):
+            nc.tensor.matmul_mx(
+                out=acc,
+                lhsT=weight_code.bitcast(FP8X4),
+                lhsT_scale=weight_scale,
+                rhs=moving_code.bitcast(FP8X4),
+                rhs_scale=moving_scale,
+                start=True,
+                stop=True,
+            )
 
         word_table = keep.tile([P, T], U32, name="word_table", align_bytes=64)
         word_rows = x_words[0].rearrange("p n t -> p (n t)").bitcast(I32)
@@ -79,8 +103,8 @@ def tile_picked_hop2_relu_p_kernel(
             nc.sync.dma_start(
                 x_scale[r:P:QUADRANT, :].bitcast(I32), picked_scale[SCALE_STEP * r : P : QUADRANT, :].bitcast(I32)
             )
-
         nc.sync.dma_start(w1_raw[1][:], w1_rows[:, :, half:])
+
         w2_raw = keep.tile([P, PACK, N], F32, name="w2_raw", align_bytes=64)
         nc.sync.dma_start(w2_raw[:], w2.rearrange("(p j) n -> p j n", j=PACK))
         gate_sb = []
@@ -88,10 +112,10 @@ def tile_picked_hop2_relu_p_kernel(
             tile = keep.tile([P, V], F32, name="gate%d" % d, align_bytes=64)
             nc.sync.dma_start(tile[:], gate[d])
             gate_sb.append(tile)
-        gate_col = keep.tile([P, HOPS, 8], F32, name="gate_col")
+        gate_col = keep.tile([P, HOPS, BLOCK_WORDS], F32, name="gate_col")
         with nc.allow_non_contiguous_dma(reason="one weight a partition"):
             for d in range(HOPS):
-                nc.sync.dma_start(gate_col[:, d, : FETCHED // P], gate[d, 0, :FETCHED].rearrange("(b v) -> v b", v=P))
+                nc.sync.dma_start(gate_col[:, d, : LOW // P], gate[d, 0, :LOW].rearrange("(b v) -> v b", v=P))
         nxt_sb = [load_list("nxt1_sb", nxt1, U), load_list("nxt2_sb", nxt2, U)]
         gate2_sb = keep.tile([P, HOPS, U], F32, name="gate2_sb")
         nc.sync.dma_start(gate2_sb[:], gate2.rearrange("d p u -> p d u"))
@@ -102,228 +126,199 @@ def tile_picked_hop2_relu_p_kernel(
         x_first = keep.tile([P, X_FIRST], U32, name="x_first", align_bytes=64)
         nc.vector.tensor_copy(x_first[:], word_table[:].indirect(entries(offs_sb, 0, X_FIRST)))
 
-        w1_bf = []
-        w1_bf2 = keep.tile([P, 2, P, PACK], BF16, name="w1_bf2", align_bytes=64)
+        w1_high = keep.tile([P, 2, P, PACK], BF16, name="w1_high", align_bytes=64)
 
-        def deal_first(copy, a):
-            w1_bf.append(keep.tile([P, P, PACK], BF16, name="w1_bf%d" % a, align_bytes=64))
+        def deal_low(copy, a):
+            tile = keep.tile([P, P, PACK], BF16, name="w1_low%d" % a, align_bytes=64)
             src = w1_raw[a][:].rearrange("p j (q u e) -> p u q j e", u=2, e=2)[:, 0]
-            copy(w1_bf[a][:].rearrange("p (q e) j -> p q j e", e=2), src)
+            copy(tile[:].rearrange("p (q e) j -> p q j e", e=2), src)
+            return tile[:].rearrange("p m j -> p (m j)")
 
-        def deal_second(copy, a):
-            src = w1_raw[a][:].rearrange("p j (c i u e) -> p u c j i e", i=2, u=2, e=2)[:, 1]
-            dst = w1_bf2[:, :, a * P // 2 : (a + 1) * P // 2, :]
-            copy(dst.rearrange("p e (c i) j -> p c j i e", i=2), src)
+        def deal_high(copy, a):
+            src = w1_raw[a][:].rearrange("p j (c s u e) -> p u c j s e", s=2, u=2, e=2)[:, 1]
+            dst = w1_high[:, :, a * P // 2 : (a + 1) * P // 2, :]
+            copy(dst.rearrange("p e (c s) j -> p c j s e", s=2), src)
 
-        def quantise_w1(name, values, width):
-            code = keep.tile([P, width], U32, name=name + "_code", tag=name + "_code", align_bytes=64)
-            scale = keep.tile([P, width], U8, name=name + "_scale", tag=name + "_scale", align_bytes=64)
-            nc.vector.quantize_mx(out=code[:].bitcast(FP8X4), scales=scale[:], in_=values)
-            return code, scale
-
-        deal_first(nc.scalar.copy, 0)
-        w1_q = [quantise_w1("w1_0", w1_bf[0][:].rearrange("p m j -> p (m j)"), P)]
+        code0, scale0 = quantise("w1_0", deal_low(nc.scalar.copy, 0), P)
         x_last = keep.tile([P, S - X_FIRST], U32, name="x_last", tag="picked", align_bytes=64)
         nc.vector.tensor_copy(x_last[:], word_table[:].indirect(entries(offs_sb, X_FIRST, S - X_FIRST)))
-        deal_second(nc.scalar.copy, 0)
-        deal_first(nc.vector.tensor_copy, 1)
-        deal_second(nc.vector.tensor_copy, 1)
-        w1_q.append(quantise_w1("w1_1", w1_bf[1][:].rearrange("p m j -> p (m j)"), P))
+        deal_high(nc.scalar.copy, 0)
+        w1_low1 = deal_low(nc.vector.tensor_copy, 1)
+        deal_high(nc.vector.tensor_copy, 1)
+        code1, scale1 = quantise("w1_1", w1_low1, P)
         w2_bf = keep.tile([P, N, PACK], BF16, name="w2_bf", align_bytes=64)
         nc.vector.tensor_copy(
-            w2_bf[:].rearrange("p (c i) j -> p c j i", i=2),
-            w2_raw[:].rearrange("p j (c i) -> p c j i", i=2),
+            w2_bf[:].rearrange("p (c s) j -> p c j s", s=2),
+            w2_raw[:].rearrange("p j (c s) -> p c j s", s=2),
         )
-        w1_q.append(quantise_w1("w1_2", w1_bf2[:].rearrange("p t m j -> p (t m j)"), 2 * P))
-        w2_code = keep.tile([P, N], U32, name="w2_code", align_bytes=64)
-        w2_scale = keep.tile([P, N], U8, name="w2_scale", align_bytes=64)
-        nc.vector.quantize_mx(
-            out=w2_code[:].bitcast(FP8X4), scales=w2_scale[:], in_=w2_bf[:].rearrange("p n j -> p (n j)")
-        )
-        w1_code = [w1_q[0][0][:], w1_q[1][0][:], w1_q[2][0][:, :P], w1_q[2][0][:, P:]]
-        w1_scale = [w1_q[0][1][:], w1_q[1][1][:], w1_q[2][1][:, :P], w1_q[2][1][:, P:]]
+        code23, scale23 = quantise("w1_23", w1_high[:].rearrange("p e m j -> p (e m j)"), 2 * P)
+        w2_code, w2_scale = quantise("w2", w2_bf[:].rearrange("p n j -> p (n j)"), N)
+        w1_code = [code0[:], code1[:], code23[:, :P], code23[:, P:]]
+        w1_scale = [scale0[:], scale1[:], scale23[:, :P], scale23[:, P:]]
 
         h = []
-        fetched = {}
 
-        def fetch(t):
-            for d in range(HOPS):
-                tag = ("w1_1_code", "w1_1_scale")[d] if t == 0 else "fetched%d" % d
-                tile = keep.tile([P, FETCHED], F32, name="fetched%d_%d" % (t, d), tag=tag, align_bytes=64)
-                nc.scalar.activation(tile[:], h[t][:].indirect(entries(pos_sb[d], 0, FETCHED)), COPY)
-                fetched[t, d] = tile
-
-        def product(acc, t, s0, count):
-            codes = x_first[:, s0 : s0 + count] if s0 < X_FIRST else x_last[:, s0 - X_FIRST : s0 - X_FIRST + count]
-            nc.tensor.matmul_mx(
-                out=acc,
-                lhsT=w1_code[t].bitcast(FP8X4),
-                lhsT_scale=w1_scale[t],
-                rhs=codes.bitcast(FP8X4),
-                rhs_scale=x_scale[:, s0 : s0 + count],
-                start=True,
-                stop=True,
-            )
+        def x_code(s0, s1):
+            return x_first[:, s0:s1] if s0 < X_FIRST else x_last[:, s0 - X_FIRST : s1 - X_FIRST]
 
         def make_h(t):
-            h_t = keep.tile([P, S], F32, name="h%d" % t, tag="h%d" % t, align_bytes=64)
-            pieces = FIRST_PIECES if t < 2 else ((0, BANK), (BANK, BANK))
-            for n, (s0, count) in enumerate(pieces):
-                acc = bank_tile([P, count], "h_acc", H_BANKS[t][n])
-                cuts = (s0, X_FIRST, s0 + count) if s0 < X_FIRST < s0 + count else (s0, s0 + count)
+            h_t = keep.tile([P, S], F32, name="h%d" % t, align_bytes=64)
+            width = H_WIDTHS[t]
+            for s0, bank in zip(range(0, S, width), H_BANKS[t]):
+                acc = bank_tile([P, width], "h_acc", bank)
+                cuts = (s0, X_FIRST, s0 + width) if s0 < X_FIRST < s0 + width else (s0, s0 + width)
                 for c0, c1 in zip(cuts, cuts[1:]):
-                    product(acc[:, c0 - s0 : c1 - s0], t, c0, c1 - c0)
-                nc.scalar.activation(h_t[:, s0 : s0 + count], acc[:], RELU)
+                    product(acc[:, c0 - s0 : c1 - s0], w1_code[t], w1_scale[t], x_code(c0, c1), x_scale[:, c0:c1])
+                nc.scalar.activation(h_t[:, s0 : s0 + width], acc[:], RELU)
             h.append(h_t)
 
-        def gather_term(dst, t, d, v0, width):
+        def gather_plain(t, tags):
+            tiles = []
+            for d in range(HOPS):
+                tile = keep.tile([P, LOW], F32, name="plain%d_%d" % (t, d), tag=tags[d], align_bytes=64)
+                nc.scalar.activation(tile[:], h[t][:].indirect(entries(pos_sb[d], 0, LOW)), COPY)
+                tiles.append(tile)
+            return tiles
+
+        make_h(0)
+        make_h(1)
+        make_h(2)
+        plain = [gather_plain(0, ("w1_1_code", "w1_1_scale"))]
+        make_h(3)
+        plain.append(gather_plain(1, ("plain_first", "plain_second")))
+
+        plain_turned = [bank_tile([P, HOPS, 2, P], "plain_turned", bank) for bank in PLAIN_BANKS]
+        sums = [bank_tile([P, 2, P], "sums", bank) for bank in SUM_BANKS]
+        high_terms = [keep.tile([P, 2, V], F32, name="high_terms%d" % d, align_bytes=64) for d in range(HOPS)]
+
+        def gather_terms(dst, t, d, v0, v1):
             nc.vector.tensor_tensor(
-                dst, h[t][:].indirect(entries(pos_sb[d], v0, width)), gate_sb[d][:, v0 : v0 + width], MULT
+                dst, h[t][:].indirect(entries(pos_sb[d], v0, v1 - v0)), gate_sb[d][:, v0:v1], MULT
             )
 
-        def pair_view(rows, u):
-            if u == 0:
-                return rows.rearrange("v a (q e) -> v (a q) e", e=2)
-            return rows.rearrange("v e p -> v p e")
-
-        def turn_terms(t, d, term, v0, blocks):
-            for blk in blocks:
+        def sum_terms(t, d, terms, groups):
+            for n, group in enumerate(groups):
                 nc.tensor.matmul(
-                    sums[blk][:, t % 2, :],
-                    term[:, blk * P - v0 : (blk + 1) * P - v0],
+                    sums[group][:, t % 2, :],
+                    terms[:, n * P : (n + 1) * P],
                     ident[:],
                     start=(d == 0),
                     stop=(d == HOPS - 1),
                     is_transpose=True,
                 )
 
-        def gather_first_pair(t):
+        def first_pair_terms(t):
             for d in range(HOPS):
-                term = keep.tile([P, V - FETCHED], F32, name="term%d_%d" % (t, d), align_bytes=64)
-                gather_term(term[:], t, d, FETCHED, V - FETCHED)
-                turn_terms(t, d, term, FETCHED, range(FETCHED // P, V // P))
+                terms = keep.tile([P, V - LOW], F32, name="low_terms%d_%d" % (t, d), align_bytes=64)
+                gather_terms(terms[:], t, d, LOW, V)
+                sum_terms(t, d, terms, high_groups)
 
-        def gather_second_pair(t, v0, v1):
+        def second_pair_terms(t):
             for d in range(HOPS):
-                gather_term(second_terms[d][:, t - 2, v0:v1], t, d, v0, v1 - v0)
-                if v0 < TURNED:
-                    turn_terms(t, d, second_terms[d][:, t - 2, :], 0, range(TURNED // P))
+                terms = high_terms[d][:, t - 2, :]
+                cut = LOW if (t, d) == (PACK - 1, HOPS - 1) else V
+                gather_terms(terms[:, :cut], t, d, 0, cut)
+                sum_terms(t, d, terms, low_groups)
+                if cut < V:
+                    gather_terms(terms[:, cut:], t, d, cut, V)
 
         def turn_plain(t):
             for d in range(HOPS):
-                for blk in range(FETCHED // P):
-                    nc.tensor.transpose(plain[blk][:, d, t, :], fetched[t, d][:, blk * P : (blk + 1) * P], ident[:])
+                for group in low_groups:
+                    nc.tensor.transpose(
+                        plain_turned[group][:, d, t, :], plain[t][d][:, group * P : (group + 1) * P], ident[:]
+                    )
 
-        z_rows = {}
-
-        def round_rows(blk, u):
-            rows = keep.tile([P, P, 2], BF16, name="z_rows%d_%d" % (blk, u), align_bytes=64)
-            nc.scalar.copy(rows[:], pair_view(sums[blk], u))
-            z_rows[blk, u] = rows
-
-        def scale_first(blk):
-            tile = keep.tile([P, P, 2], F32, name="scaled%d" % blk, align_bytes=64)
-            nc.scalar.activation(tile[:], pair_view(plain[blk][:, 0], 0), COPY, scale=gate_col[:, 0, blk : blk + 1])
-            return tile
-
-        def add_second(blk, scaled):
-            rows = keep.tile([P, P, 2], BF16, name="z_rows%d_0" % blk, align_bytes=64)
-            nc.vector.scalar_tensor_tensor(
-                rows[:], pair_view(plain[blk][:, 1], 0), gate_col[:, 1, blk : blk + 1], scaled[:], MULT, ADD
-            )
-            z_rows[blk, 0] = rows
-
-        def turn_back(blk, u, back):
-            nc.tensor.transpose(back, z_rows[blk, u][:].rearrange("v p e -> v (p e)").bitcast(F32), ident[:])
-
-        make_h(0)
-        make_h(1)
-        make_h(2)
-        fetch(0)
-        make_h(3)
-        fetch(1)
-        plain = [bank_tile([P, HOPS, 2, P], "z_plain", bank) for bank in (4, 5)]
-        sums = [bank_tile([P, 2, P], "z_sum", bank)[:] for bank in (0, 1, 6, 7)]
-        second_terms = [keep.tile([P, 2, V], F32, name="second_terms%d" % d, align_bytes=64) for d in range(HOPS)]
-        gather_first_pair(0)
-        gather_first_pair(1)
+        first_pair_terms(0)
+        first_pair_terms(1)
         turn_plain(0)
-        gather_second_pair(2, 0, V)
+        second_pair_terms(2)
         turn_plain(1)
-        gather_second_pair(3, 0, TURNED)
-        gather_second_pair(3, TURNED, V)
-        late_back = bank_tile([P, 2, P], "z_back_late", 2)
-        for blk in (2, 3):
-            round_rows(blk, 0)
-            turn_back(blk, 0, late_back[:, blk - 2, :])
-        scaled = [scale_first(blk) for blk in range(2)]
-        early_back = [bank_tile([P, 2, P], "z_back", bank) for bank in (3, 6)]
-        for blk in range(2):
-            round_rows(blk, 1)
-            turn_back(blk, 1, early_back[blk][:, 1, :])
-        for blk in range(2):
-            add_second(blk, scaled[blk])
-            turn_back(blk, 0, early_back[blk][:, 0, :])
-        z_late = []
-        for b in range(2):
-            tile = keep.tile([P, P * PACK], BF16, name="z_late%d" % b, align_bytes=64)
-            nc.scalar.copy(tile[:].bitcast(F32).rearrange("p (v u) -> p v u", u=2)[:, :, 0], late_back[:, b, :])
-            z_late.append(tile)
+        second_pair_terms(3)
 
-        g = keep.tile([P, V], F32, name="g")
+        def in_pair_order(turned, u):
+            if u == 0:
+                return turned.rearrange("v a (q e) -> v (a q) e", e=2)
+            return turned.rearrange("v e p -> v p e")
 
-        def second_product(blk, z_bf, bank, on_vector):
-            z_code = keep.tile([P, P], U32, name="z_code%d" % blk, align_bytes=64)
-            z_scale = keep.tile([P, P], U8, name="z_scale%d" % blk, align_bytes=64)
-            nc.vector.quantize_mx(out=z_code[:].bitcast(FP8X4), scales=z_scale[:], in_=z_bf[:])
-            g_acc = bank_tile([P, P], "g_acc", bank)
-            nc.tensor.matmul_mx(
-                out=g_acc[:],
-                lhsT=w2_code[:].bitcast(FP8X4),
-                lhsT_scale=w2_scale[:],
-                rhs=z_code[:].bitcast(FP8X4),
-                rhs_scale=z_scale[:],
-                start=True,
-                stop=True,
+        def rows_tile(group, u):
+            return keep.tile([P, P, 2], BF16, name="rows%d_%d" % (group, u), align_bytes=64)
+
+        def turn_back(rows, back):
+            nc.tensor.transpose(back, rows[:].rearrange("v p e -> v (p e)").bitcast(F32), ident[:])
+
+        def round_sums(group, u, back):
+            rows = rows_tile(group, u)
+            nc.scalar.copy(rows[:], in_pair_order(sums[group][:], u))
+            turn_back(rows, back)
+
+        high_back = bank_tile([P, len(high_groups), P], "high_back", HIGH_BACK_BANK)
+        for n, group in enumerate(high_groups):
+            round_sums(group, 0, high_back[:, n, :])
+        scaled = []
+        for group in low_groups:
+            tile = keep.tile([P, P, 2], F32, name="scaled%d" % group, align_bytes=64)
+            nc.scalar.activation(
+                tile[:], in_pair_order(plain_turned[group][:, 0], 0), COPY, scale=gate_col[:, 0, group : group + 1]
             )
-            cols = g[:, blk * P : (blk + 1) * P]
-            if on_vector:
-                nc.vector.tensor_scalar_max(cols, g_acc[:], 0.0)
-            else:
-                nc.scalar.activation(cols, g_acc[:], RELU)
-
-        for b in range(2):
-            cols = slice(TURNED + b * P, TURNED + (b + 1) * P)
-            nc.vector.tensor_tensor(
-                z_late[b][:].rearrange("p (c i u e) -> p c u e i", i=2, u=2, e=2)[:, :, 1],
-                second_terms[0][:, :, cols].rearrange("p e (c i) -> p c e i", i=2),
-                second_terms[1][:, :, cols].rearrange("p e (c i) -> p c e i", i=2),
+            scaled.append(tile)
+        low_back = [bank_tile([P, 2, P], "low_back", bank) for bank in LOW_BACK_BANKS]
+        for group in low_groups:
+            round_sums(group, 1, low_back[group][:, 1, :])
+        for group in low_groups:
+            rows = rows_tile(group, 0)
+            nc.vector.scalar_tensor_tensor(
+                rows[:],
+                in_pair_order(plain_turned[group][:, 1], 0),
+                gate_col[:, 1, group : group + 1],
+                scaled[group][:],
+                MULT,
                 ADD,
             )
-        z_early = []
-        for blk in range(2):
-            tile = keep.tile([P, P * PACK], BF16, name="z_early%d" % blk, align_bytes=64)
-            nc.scalar.copy(
-                tile[:].bitcast(F32).rearrange("p (v u) -> p v u", u=2),
-                early_back[blk][:].rearrange("p u v -> p v u"),
+            turn_back(rows, low_back[group][:, 0, :])
+
+        z_bf = {}
+
+        def z_pairs(group):
+            z_bf[group] = keep.tile([P, P * PACK], BF16, name="z_bf%d" % group, align_bytes=64)
+            return z_bf[group][:].bitcast(F32).rearrange("p (v u) -> p v u", u=2)
+
+        for n, group in enumerate(high_groups):
+            nc.scalar.copy(z_pairs(group)[:, :, 0], high_back[:, n, :])
+        g = keep.tile([P, V], F32, name="g")
+        for group in high_groups:
+            cols = slice(group * P, (group + 1) * P)
+            nc.vector.tensor_tensor(
+                z_bf[group][:].rearrange("p (c s u e) -> p c u e s", s=2, u=2, e=2)[:, :, 1],
+                high_terms[0][:, :, cols].rearrange("p e (c s) -> p c e s", s=2),
+                high_terms[1][:, :, cols].rearrange("p e (c s) -> p c e s", s=2),
+                ADD,
             )
-            z_early.append(tile)
-        second_product(2, z_late[0], 7, False)
-        second_product(3, z_late[1], 0, False)
-        second_product(0, z_early[0], 1, False)
-        second_product(1, z_early[1], 4, True)
+        for group in low_groups:
+            nc.scalar.copy(z_pairs(group), low_back[group][:].rearrange("p u v -> p v u"))
+
+        order = list(high_groups) + list(low_groups)
+        for group in order:
+            z_code, z_scale = quantise("z%d" % group, z_bf[group][:], P)
+            acc = bank_tile([P, P], "g_acc", G_BANKS[group])
+            product(acc[:], w2_code[:], w2_scale[:], z_code[:], z_scale[:])
+            cols = g[:, group * P : (group + 1) * P]
+            if group == order[-2]:
+                nc.vector.tensor_scalar_max(cols, acc[:], 0.0)
+            else:
+                nc.scalar.activation(cols, acc[:], RELU)
 
         count = U // 2
         halves = [slice(a * count, (a + 1) * count) for a in range(2)]
         second = keep.tile([P, U], F32, name="root_second")
-        for a in range(2):
-            nc.scalar.activation(second[:, halves[a]], g[:].indirect(entries(nxt_sb[1], a * count, count)), COPY)
-        first = keep.tile([P, U], F32, name="root_first")
-        nc.vector.tensor_tensor(first[:], g[:].indirect(nxt_sb[0][:]), gate2_sb[:, 0, :], MULT)
-        weighed = keep.tile([P, U], F32, name="root_weighed")
         for cols in halves:
-            nc.vector.tensor_tensor(weighed[:, cols], second[:, cols], gate2_sb[:, 1, cols], MULT)
+            nc.scalar.activation(second[:, cols], g[:].indirect(entries(nxt_sb[1], cols.start, count)), COPY)
+        first_term = keep.tile([P, U], F32, name="root_first_term")
+        nc.vector.tensor_tensor(first_term[:], g[:].indirect(nxt_sb[0][:]), gate2_sb[:, 0, :], MULT)
+        second_term = keep.tile([P, U], F32, name="root_second_term")
+        for cols in halves:
+            nc.vector.tensor_tensor(second_term[:, cols], second[:, cols], gate2_sb[:, 1, cols], MULT)
         for a, cols in enumerate(halves):
             result = keep.tile([P, count], F32, name="result%d" % a)
-            nc.vector.tensor_tensor(result[:], first[:, cols], weighed[:, cols], ADD)
+            nc.vector.tensor_tensor(result[:], first_term[:, cols], second_term[:, cols], ADD)
             nc.sync.dma_start(out[:, cols], result[:])

@@ -82,7 +82,7 @@ def tile_picked_hop2_relu_p_kernel(
         word_rows = x_words[0].rearrange("p n t -> p (n t)").bitcast(I32)
         nc.sync.dma_start(word_table[:, :X_LEAD].bitcast(I32), word_rows[:, :X_LEAD])
         offs_sb = load_list("offs_sb", offs, S)
-        pos_sb = [load_list("pos1_sb", pos1, V)]
+        pos_sb = [load_list("pos1_sb", pos1, V), load_list("pos2_sb", pos2, V)]
 
         scale_table = keep.tile([P, T], U8, name="scale_table", tag="scale_table", align_bytes=64)
         nc.vector.memset(scale_table[:].bitcast(I32), 0)
@@ -91,9 +91,14 @@ def tile_picked_hop2_relu_p_kernel(
 
         w1_rows = w1.rearrange("(p j) c -> p j c", j=PACK)
         half = H // 2
-        w1_raw = [keep.tile([P, PACK, half], F32, name="w1_raw%d" % a) for a in range(2)]
-        nc.sync.dma_start(w1_raw[0][:], w1_rows[:, :, :half])
-        pos_sb.append(load_list("pos2_sb", pos2, V))
+        parts = ((0, half), (half, P), (half + P, P))
+        w1_raw = [keep.tile([P, PACK, width], F32, name="w1_raw%d" % c0) for c0, width in parts]
+
+        def load_w1(n):
+            nc.sync.dma_start(w1_raw[n][:], w1_rows[:, :, parts[n][0] : parts[n][0] + parts[n][1]])
+
+        load_w1(0)
+        load_w1(1)
 
         x_scale = keep.tile([P, S], U8, name="x_scale", align_bytes=64)
         nc.vector.memset(x_scale[:].bitcast(I32), 0)
@@ -103,7 +108,7 @@ def tile_picked_hop2_relu_p_kernel(
             nc.sync.dma_start(
                 x_scale[r:P:QUADRANT, :].bitcast(I32), picked_scale[SCALE_STEP * r : P : QUADRANT, :].bitcast(I32)
             )
-        nc.sync.dma_start(w1_raw[1][:], w1_rows[:, :, half:])
+        load_w1(2)
 
         w2_raw = keep.tile([P, PACK, N], F32, name="w2_raw", align_bytes=64)
         nc.sync.dma_start(w2_raw[:], w2.rearrange("(p j) n -> p j n", j=PACK))
@@ -128,24 +133,30 @@ def tile_picked_hop2_relu_p_kernel(
 
         w1_high = keep.tile([P, 2, P, PACK], BF16, name="w1_high", align_bytes=64)
 
-        def deal_low(copy, a):
-            tile = keep.tile([P, P, PACK], BF16, name="w1_low%d" % a, align_bytes=64)
-            src = w1_raw[a][:].rearrange("p j (q u e) -> p u q j e", u=2, e=2)[:, 0]
-            copy(tile[:].rearrange("p (q e) j -> p q j e", e=2), src)
-            return tile[:].rearrange("p m j -> p (m j)")
+        w1_low = [keep.tile([P, P, PACK], BF16, name="w1_low%d" % a, align_bytes=64) for a in range(2)]
 
-        def deal_high(copy, a):
-            src = w1_raw[a][:].rearrange("p j (c s u e) -> p u c j s e", s=2, u=2, e=2)[:, 1]
-            dst = w1_high[:, :, a * P // 2 : (a + 1) * P // 2, :]
+        def deal_low(copy, n):
+            c0, width = parts[n]
+            src = w1_raw[n][:].rearrange("p j (q u e) -> p u q j e", u=2, e=2)[:, 0]
+            dst = w1_low[c0 // half][:, c0 % half // 2 : (c0 % half + width) // 2, :]
+            copy(dst.rearrange("p (q e) j -> p q j e", e=2), src)
+
+        def deal_high(copy, n):
+            c0, width = parts[n]
+            src = w1_raw[n][:].rearrange("p j (c s u e) -> p u c j s e", s=2, u=2, e=2)[:, 1]
+            dst = w1_high[:, :, c0 // PACK : (c0 + width) // PACK, :]
             copy(dst.rearrange("p e (c s) j -> p c j s e", s=2), src)
 
-        code0, scale0 = quantise("w1_0", deal_low(nc.scalar.copy, 0), P)
+        deal_low(nc.scalar.copy, 0)
+        code0, scale0 = quantise("w1_0", w1_low[0][:].rearrange("p m j -> p (m j)"), P)
         x_last = keep.tile([P, S - X_FIRST], U32, name="x_last", tag="picked", align_bytes=64)
         nc.vector.tensor_copy(x_last[:], word_table[:].indirect(entries(offs_sb, X_FIRST, S - X_FIRST)))
         deal_high(nc.scalar.copy, 0)
-        w1_low1 = deal_low(nc.vector.tensor_copy, 1)
-        deal_high(nc.vector.tensor_copy, 1)
-        code1, scale1 = quantise("w1_1", w1_low1, P)
+        deal_low(nc.scalar.copy, 1)
+        deal_high(nc.scalar.copy, 1)
+        deal_low(nc.vector.tensor_copy, 2)
+        deal_high(nc.vector.tensor_copy, 2)
+        code1, scale1 = quantise("w1_1", w1_low[1][:].rearrange("p m j -> p (m j)"), P)
         w2_bf = keep.tile([P, N, PACK], BF16, name="w2_bf", align_bytes=64)
         nc.vector.tensor_copy(
             w2_bf[:].rearrange("p (c s) j -> p c j s", s=2),

@@ -23,7 +23,9 @@ PACK = 4
 HOPS = 2
 STRIPE = 16
 QUADRANT = 32
-SCALE_STEP = 8
+SCALE_STEP = 4
+SCALE_FIRST, SCALE_END = 32, 96
+SCALE_ROWS = 4
 BANK = 512
 BLOCK_WORDS = 8
 
@@ -82,11 +84,11 @@ def tile_picked_hop2_relu_p_kernel(
         word_rows = x_words[0].rearrange("p n t -> p (n t)").bitcast(I32)
         nc.sync.dma_start(word_table[:, :X_LEAD].bitcast(I32), word_rows[:, :X_LEAD])
         offs_sb = load_list("offs_sb", offs, S)
-        pos_sb = [load_list("pos1_sb", pos1, V), load_list("pos2_sb", pos2, V)]
+        pos_sb = [load_list("pos1_sb", pos1, V)]
 
         scale_table = keep.tile([P, T], U8, name="scale_table", tag="scale_table", align_bytes=64)
         nc.vector.memset(scale_table[:].bitcast(I32), 0)
-        nc.sync.dma_start(scale_table[0:P:SCALE_STEP, :].bitcast(I32), x_scales[0].bitcast(I32))
+        nc.sync.dma_start(scale_table[SCALE_FIRST:SCALE_END:SCALE_STEP, :].bitcast(I32), x_scales[0].bitcast(I32))
         nc.sync.dma_start(word_table[:, X_LEAD:].bitcast(I32), word_rows[:, X_LEAD:])
 
         w1_rows = w1.rearrange("(p j) c -> p j c", j=PACK)
@@ -104,19 +106,18 @@ def tile_picked_hop2_relu_p_kernel(
         nc.vector.memset(x_scale[:].bitcast(I32), 0)
         picked_scale = keep.tile([P, S], U8, name="picked_scale", tag="picked", align_bytes=64)
         nc.vector.tensor_copy(picked_scale[:], scale_table[:].indirect(offs_sb[:]))
-        for r in range(QUADRANT // SCALE_STEP):
-            nc.sync.dma_start(
-                x_scale[r:P:QUADRANT, :].bitcast(I32), picked_scale[SCALE_STEP * r : P : QUADRANT, :].bitcast(I32)
-            )
+        for r in range(SCALE_ROWS):
+            rows_r = slice(SCALE_FIRST + SCALE_STEP * r, SCALE_END, SCALE_STEP * SCALE_ROWS)
+            nc.sync.dma_start(x_scale[r:P:QUADRANT, :].bitcast(I32), picked_scale[rows_r, :].bitcast(I32))
+        pos_sb.append(load_list("pos2_sb", pos2, V))
         load_w1(2)
 
         w2_raw = keep.tile([P, PACK, N], F32, name="w2_raw", align_bytes=64)
         nc.sync.dma_start(w2_raw[:], w2.rearrange("(p j) n -> p j n", j=PACK))
-        gate_sb = []
-        for d in range(HOPS):
-            tile = keep.tile([P, V], F32, name="gate%d" % d, align_bytes=64)
-            nc.sync.dma_start(tile[:], gate[d])
-            gate_sb.append(tile)
+        gate_rows = gate.rearrange("d p v -> p d v")
+        gate_sb = keep.tile([P, HOPS, V], F32, name="gate_sb", align_bytes=64)
+        nc.sync.dma_start(gate_sb[:, :, LOW:], gate_rows[:, :, LOW:])
+        nc.sync.dma_start(gate_sb[:, :, :LOW], gate_rows[:, :, :LOW])
         gate_col = keep.tile([P, HOPS, BLOCK_WORDS], F32, name="gate_col")
         with nc.allow_non_contiguous_dma(reason="one weight a partition"):
             for d in range(HOPS):
@@ -204,7 +205,7 @@ def tile_picked_hop2_relu_p_kernel(
 
         def gather_terms(dst, t, d, v0, v1):
             nc.vector.tensor_tensor(
-                dst, h[t][:].indirect(entries(pos_sb[d], v0, v1 - v0)), gate_sb[d][:, v0:v1], MULT
+                dst, h[t][:].indirect(entries(pos_sb[d], v0, v1 - v0)), gate_sb[:, d, v0:v1], MULT
             )
 
         def sum_terms(t, d, terms, groups):

@@ -29,7 +29,7 @@ SCALE_ROWS = 4
 BANK = 512
 BLOCK_WORDS = 8
 
-X_LEAD = 768
+X_LEAD = 1280
 X_FIRST = 768
 LOW = 256
 H_WIDTHS = (256, 256, BANK, BANK)

@@ -200,7 +200,7 @@ def tile_picked_hop2_relu_p_kernel(
         plain.append(gather_plain(1, ("plain_first", "plain_second")))
 
         plain_turned = [bank_tile([P, HOPS, 2, P], "plain_turned", bank) for bank in PLAIN_BANKS]
-        sums = [bank_tile([P, 2, P], "sums", bank) for bank in SUM_BANKS]
+        sums = [bank_tile([P, 2, P], "sums", bank) for bank in SUM_BANKS[:2]]
         high_terms = [keep.tile([P, 2, V], F32, name="high_terms%d" % d, align_bytes=64) for d in range(HOPS)]
 
         def gather_terms(dst, t, d, v0, v1):
@@ -219,11 +219,24 @@ def tile_picked_hop2_relu_p_kernel(
                     is_transpose=True,
                 )
 
+        high_sums = bank_tile([P, len(high_groups), 2, P], "high_sums", SUM_BANKS[2])
+
         def first_pair_terms(t):
+            tiles = []
             for d in range(HOPS):
                 terms = keep.tile([P, V - LOW], F32, name="low_terms%d_%d" % (t, d), align_bytes=64)
                 gather_terms(terms[:], t, d, LOW, V)
-                sum_terms(t, d, terms, high_groups)
+                tiles.append(terms)
+            for n in range(len(high_groups)):
+                for d in range(HOPS):
+                    nc.tensor.matmul(
+                        high_sums[:, n, t, :],
+                        tiles[d][:, n * P : (n + 1) * P],
+                        ident[:],
+                        start=(d == 0),
+                        stop=(d == HOPS - 1),
+                        is_transpose=True,
+                    )
 
         def second_pair_terms(t):
             for d in range(HOPS):
@@ -265,8 +278,10 @@ def tile_picked_hop2_relu_p_kernel(
             turn_back(rows, back)
 
         high_back = bank_tile([P, len(high_groups), P], "high_back", HIGH_BACK_BANK)
-        for n, group in enumerate(high_groups):
-            round_sums(group, 0, high_back[:, n, :])
+        high_rows = keep.tile([P, len(high_groups), 2 * P], BF16, name="high_rows", align_bytes=64)
+        nc.scalar.copy(high_rows[:].rearrange("v g c -> v (g c)"), high_sums[:].rearrange("v g a m -> v (g a m)"))
+        for n in range(len(high_groups)):
+            nc.tensor.transpose(high_back[:, n, :], high_rows[:, n, :].bitcast(F32), ident[:])
         scaled = []
         for group in low_groups:
             tile = keep.tile([P, P, 2], F32, name="scaled%d" % group, align_bytes=64)
@@ -295,42 +310,56 @@ def tile_picked_hop2_relu_p_kernel(
             z_bf[group] = keep.tile([P, P * PACK], BF16, name="z_bf%d" % group, align_bytes=64)
             return z_bf[group][:].bitcast(F32).rearrange("p (v u) -> p v u", u=2)
 
+        z_high = keep.tile([P, len(high_groups), P * PACK], BF16, name="z_high", align_bytes=64)
+        nc.scalar.copy(
+            z_high[:].rearrange("p g c -> p (g c)").bitcast(F32).rearrange("p (v u) -> p v u", u=2)[:, :, 0],
+            high_back[:].rearrange("p g v -> p (g v)"),
+        )
         for n, group in enumerate(high_groups):
-            nc.scalar.copy(z_pairs(group)[:, :, 0], high_back[:, n, :])
+            z_bf[group] = z_high[:, n, :]
         g = keep.tile([P, V], F32, name="g")
         for group in high_groups:
             cols = slice(group * P, (group + 1) * P)
             nc.vector.tensor_tensor(
-                z_bf[group][:].rearrange("p (c s u e) -> p c u e s", s=2, u=2, e=2)[:, :, 1],
+                z_bf[group].rearrange("p (c s u e) -> p c u e s", s=2, u=2, e=2)[:, :, 1],
                 high_terms[0][:, :, cols].rearrange("p e (c s) -> p c e s", s=2),
                 high_terms[1][:, :, cols].rearrange("p e (c s) -> p c e s", s=2),
                 ADD,
             )
-        for group in low_groups:
-            nc.scalar.copy(z_pairs(group), low_back[group][:].rearrange("p u v -> p v u"))
+        nc.scalar.copy(z_pairs(0), low_back[0][:].rearrange("p u v -> p v u"))
+        last = [keep.tile([P, P // 2 * PACK], BF16, name="z_last%d" % a, align_bytes=64) for a in range(2)]
+        for a in range(2):
+            nc.scalar.copy(
+                last[a][:].bitcast(F32).rearrange("p (v u) -> p v u", u=2),
+                low_back[1][:, :, a * P // 2 : (a + 1) * P // 2].rearrange("p u v -> p v u"),
+            )
 
-        order = list(high_groups) + list(low_groups)
-        for group in order:
-            z_code, z_scale = quantise("z%d" % group, z_bf[group][:], P)
-            acc = bank_tile([P, P], "g_acc", G_BANKS[group])
+        parts_of_z = [(group * P, P, z_bf[group][:], G_BANKS[group]) for group in (2, 3, 0)]
+        parts_of_z.extend([(P, P // 2, last[0][:], G_BANKS[1]), (P + P // 2, P // 2, last[1][:], 5)])
+        for n, (v0, width, values, bank) in enumerate(parts_of_z):
+            z_code, z_scale = quantise("z%d" % v0, values, width)
+            acc = bank_tile([P, width], "g_acc", bank)
             product(acc[:], w2_code[:], w2_scale[:], z_code[:], z_scale[:])
-            cols = g[:, group * P : (group + 1) * P]
-            if group == order[-2]:
+            cols = g[:, v0 : v0 + width]
+            if n == 3:
                 nc.vector.tensor_scalar_max(cols, acc[:], 0.0)
             else:
                 nc.scalar.activation(cols, acc[:], RELU)
 
-        count = U // 2
-        halves = [slice(a * count, (a + 1) * count) for a in range(2)]
+        pieces = [slice(0, 96), slice(96, 192), slice(192, U)]
         second = keep.tile([P, U], F32, name="root_second")
-        for cols in halves:
-            nc.scalar.activation(second[:, cols], g[:].indirect(entries(nxt_sb[1], cols.start, count)), COPY)
+        for cols in pieces:
+            nc.scalar.activation(
+                second[:, cols], g[:].indirect(entries(nxt_sb[1], cols.start, cols.stop - cols.start)), COPY
+            )
         first_term = keep.tile([P, U], F32, name="root_first_term")
         nc.vector.tensor_tensor(first_term[:], g[:].indirect(nxt_sb[0][:]), gate2_sb[:, 0, :], MULT)
         second_term = keep.tile([P, U], F32, name="root_second_term")
-        for cols in halves:
+        for cols in pieces:
             nc.vector.tensor_tensor(second_term[:, cols], second[:, cols], gate2_sb[:, 1, cols], MULT)
-        for a, cols in enumerate(halves):
-            result = keep.tile([P, count], F32, name="result%d" % a)
-            nc.vector.tensor_tensor(result[:], first_term[:, cols], second_term[:, cols], ADD)
-            nc.sync.dma_start(out[:, cols], result[:])
+        result = keep.tile([P, U], F32, name="result", align_bytes=64)
+        for a, cols in enumerate(pieces):
+            nc.vector.tensor_tensor(result[:, cols], first_term[:, cols], second_term[:, cols], ADD)
+            if a > 0:
+                stored = slice(0 if a == 1 else cols.start, cols.stop)
+                nc.sync.dma_start(out[:, stored], result[:, stored])

@@ -346,7 +346,7 @@ def tile_picked_hop2_relu_p_kernel(
             else:
                 nc.scalar.activation(cols, acc[:], RELU)
 
-        pieces = [slice(0, 96), slice(96, 192), slice(192, U)]
+        pieces = [slice(0, U // 2), slice(U // 2, U)]
         second = keep.tile([P, U], F32, name="root_second")
         for cols in pieces:
             nc.scalar.activation(
@@ -360,6 +360,4 @@ def tile_picked_hop2_relu_p_kernel(
         result = keep.tile([P, U], F32, name="result", align_bytes=64)
         for a, cols in enumerate(pieces):
             nc.vector.tensor_tensor(result[:, cols], first_term[:, cols], second_term[:, cols], ADD)
-            if a > 0:
-                stored = slice(0 if a == 1 else cols.start, cols.stop)
-                nc.sync.dma_start(out[:, stored], result[:, stored])
+            nc.sync.dma_start(out[:, cols], result[:, cols])

@@ -32,13 +32,12 @@ BLOCK_WORDS = 8
 X_LEAD = 1280
 X_FIRST = 768
 LOW = 256
+HIGH = V - LOW
 H_WIDTHS = (256, 256, BANK, BANK)
 H_BANKS = ((0, 1, 2, 3), (4, 5, 6, 7), (0, 1), (2, 3))
 PLAIN_BANKS = (4, 5)
-SUM_BANKS = (0, 1, 6, 7)
-LOW_BACK_BANKS = (3, 6)
-HIGH_BACK_BANK = 2
-G_BANKS = (1, 4, 7, 0)
+SUM_BANKS = (0, 1)
+BACK_BANKS = (3, 6)
 
 
 def tile_picked_hop2_relu_p_kernel(
@@ -46,7 +45,6 @@ def tile_picked_hop2_relu_p_kernel(
 ):
     nc = tc.nc
     low_groups = range(LOW // P)
-    high_groups = range(LOW // P, V // P)
     with ExitStack() as ctx:
         lists = ctx.enter_context(tc.tile_pool(name="lists", bufs=1))
         keep = ctx.enter_context(tc.tile_pool(name="keep", bufs=1))
@@ -199,53 +197,22 @@ def tile_picked_hop2_relu_p_kernel(
         make_h(3)
         plain.append(gather_plain(1, ("plain_first", "plain_second")))
 
-        plain_turned = [bank_tile([P, HOPS, 2, P], "plain_turned", bank) for bank in PLAIN_BANKS]
-        sums = [bank_tile([P, 2, P], "sums", bank) for bank in SUM_BANKS[:2]]
-        high_terms = [keep.tile([P, 2, V], F32, name="high_terms%d" % d, align_bytes=64) for d in range(HOPS)]
 
         def gather_terms(dst, t, d, v0, v1):
             nc.vector.tensor_tensor(
                 dst, h[t][:].indirect(entries(pos_sb[d], v0, v1 - v0)), gate_sb[:, d, v0:v1], MULT
             )
 
-        def sum_terms(t, d, terms, groups):
-            for n, group in enumerate(groups):
-                nc.tensor.matmul(
-                    sums[group][:, t % 2, :],
-                    terms[:, n * P : (n + 1) * P],
-                    ident[:],
-                    start=(d == 0),
-                    stop=(d == HOPS - 1),
-                    is_transpose=True,
-                )
-
-        high_sums = bank_tile([P, len(high_groups), 2, P], "high_sums", SUM_BANKS[2])
-
-        def first_pair_terms(t):
-            tiles = []
+        terms = keep.tile([P, PACK, HOPS, V], F32, name="terms", align_bytes=64)
+        for a in range(2):
+            early = keep.tile([P, HOPS, HIGH], F32, name="early%d" % a, align_bytes=64)
             for d in range(HOPS):
-                terms = keep.tile([P, V - LOW], F32, name="low_terms%d_%d" % (t, d), align_bytes=64)
-                gather_terms(terms[:], t, d, LOW, V)
-                tiles.append(terms)
-            for n in range(len(high_groups)):
-                for d in range(HOPS):
-                    nc.tensor.matmul(
-                        high_sums[:, n, t, :],
-                        tiles[d][:, n * P : (n + 1) * P],
-                        ident[:],
-                        start=(d == 0),
-                        stop=(d == HOPS - 1),
-                        is_transpose=True,
-                    )
+                gather_terms(early[:, d, :], a, d, LOW, V)
+            for e in range(2):
+                nc.sync.dma_start(terms[a * P // 2 : (a + 1) * P // 2, e, :, LOW:], early[e:P:2, :, :])
 
-        def second_pair_terms(t):
-            for d in range(HOPS):
-                terms = high_terms[d][:, t - 2, :]
-                cut = LOW if (t, d) == (PACK - 1, HOPS - 1) else V
-                gather_terms(terms[:, :cut], t, d, 0, cut)
-                sum_terms(t, d, terms, low_groups)
-                if cut < V:
-                    gather_terms(terms[:, cut:], t, d, cut, V)
+        plain_turned = [bank_tile([P, HOPS, 2, P], "plain_turned", bank) for bank in PLAIN_BANKS]
+        sums = [bank_tile([P, 2, P], "sums", bank) for bank in SUM_BANKS]
 
         def turn_plain(t):
             for d in range(HOPS):
@@ -254,89 +221,72 @@ def tile_picked_hop2_relu_p_kernel(
                         plain_turned[group][:, d, t, :], plain[t][d][:, group * P : (group + 1) * P], ident[:]
                     )
 
-        first_pair_terms(0)
-        first_pair_terms(1)
+        def sum_terms(t, d):
+            for group in low_groups:
+                nc.tensor.matmul(
+                    sums[group][:, t - 2, :],
+                    terms[:, t, d, group * P : (group + 1) * P],
+                    ident[:],
+                    start=(d == 0),
+                    stop=(d == HOPS - 1),
+                    is_transpose=True,
+                )
+
         turn_plain(0)
-        second_pair_terms(2)
+        for d in range(HOPS):
+            gather_terms(terms[:, 2, d, :], 2, d, 0, V)
+            sum_terms(2, d)
         turn_plain(1)
-        second_pair_terms(3)
+        for d in range(HOPS):
+            gather_terms(terms[:, 3, d, :LOW], 3, d, 0, LOW)
+            sum_terms(3, d)
+        gather_terms(terms[:, 3, 0, LOW:], 3, 0, LOW, V)
+        late = keep.tile([P, HIGH], F32, name="late", align_bytes=64)
+        nc.scalar.activation(late[:], h[3][:].indirect(entries(pos_sb[1], LOW, HIGH)), COPY)
+        nc.vector.tensor_tensor(terms[:, 3, 1, LOW:], late[:], gate_sb[:, 1, LOW:], MULT)
 
-        def in_pair_order(turned, u):
-            if u == 0:
-                return turned.rearrange("v a (q e) -> v (a q) e", e=2)
-            return turned.rearrange("v e p -> v p e")
-
-        def rows_tile(group, u):
-            return keep.tile([P, P, 2], BF16, name="rows%d_%d" % (group, u), align_bytes=64)
+        def first_pair(group, d):
+            return plain_turned[group][:, d].rearrange("v a m -> v (a m)")
 
         def turn_back(rows, back):
-            nc.tensor.transpose(back, rows[:].rearrange("v p e -> v (p e)").bitcast(F32), ident[:])
+            nc.tensor.transpose(back, rows[:].bitcast(F32), ident[:])
 
-        def round_sums(group, u, back):
-            rows = rows_tile(group, u)
-            nc.scalar.copy(rows[:], in_pair_order(sums[group][:], u))
-            turn_back(rows, back)
-
-        high_back = bank_tile([P, len(high_groups), P], "high_back", HIGH_BACK_BANK)
-        high_rows = keep.tile([P, len(high_groups), 2 * P], BF16, name="high_rows", align_bytes=64)
-        nc.scalar.copy(high_rows[:].rearrange("v g c -> v (g c)"), high_sums[:].rearrange("v g a m -> v (g a m)"))
-        for n in range(len(high_groups)):
-            nc.tensor.transpose(high_back[:, n, :], high_rows[:, n, :].bitcast(F32), ident[:])
         scaled = []
         for group in low_groups:
-            tile = keep.tile([P, P, 2], F32, name="scaled%d" % group, align_bytes=64)
-            nc.scalar.activation(
-                tile[:], in_pair_order(plain_turned[group][:, 0], 0), COPY, scale=gate_col[:, 0, group : group + 1]
-            )
+            tile = keep.tile([P, 2 * P], F32, name="scaled%d" % group, align_bytes=64)
+            nc.scalar.activation(tile[:], first_pair(group, 0), COPY, scale=gate_col[:, 0, group : group + 1])
             scaled.append(tile)
-        low_back = [bank_tile([P, 2, P], "low_back", bank) for bank in LOW_BACK_BANKS]
+        back = [bank_tile([P, 2, P], "back", bank) for bank in BACK_BANKS]
         for group in low_groups:
-            round_sums(group, 1, low_back[group][:, 1, :])
+            rows = keep.tile([P, 2 * P], BF16, name="rows%d_1" % group, align_bytes=64)
+            nc.scalar.copy(rows[:].rearrange("v (p e) -> v p e", e=2), sums[group][:].rearrange("v e p -> v p e"))
+            turn_back(rows, back[group][:, 1, :])
         for group in low_groups:
-            rows = rows_tile(group, 0)
+            rows = keep.tile([P, 2 * P], BF16, name="rows%d_0" % group, align_bytes=64)
             nc.vector.scalar_tensor_tensor(
-                rows[:],
-                in_pair_order(plain_turned[group][:, 1], 0),
-                gate_col[:, 1, group : group + 1],
-                scaled[group][:],
-                MULT,
-                ADD,
+                rows[:], first_pair(group, 1), gate_col[:, 1, group : group + 1], scaled[group][:], MULT, ADD
             )
-            turn_back(rows, low_back[group][:, 0, :])
+            turn_back(rows, back[group][:, 0, :])
 
-        z_bf = {}
-
-        def z_pairs(group):
-            z_bf[group] = keep.tile([P, P * PACK], BF16, name="z_bf%d" % group, align_bytes=64)
-            return z_bf[group][:].bitcast(F32).rearrange("p (v u) -> p v u", u=2)
-
-        z_high = keep.tile([P, len(high_groups), P * PACK], BF16, name="z_high", align_bytes=64)
-        nc.scalar.copy(
-            z_high[:].rearrange("p g c -> p (g c)").bitcast(F32).rearrange("p (v u) -> p v u", u=2)[:, :, 0],
-            high_back[:].rearrange("p g v -> p (g v)"),
-        )
-        for n, group in enumerate(high_groups):
-            z_bf[group] = z_high[:, n, :]
-        g = keep.tile([P, V], F32, name="g")
-        for group in high_groups:
+        z_bf = [keep.tile([P, P * PACK], BF16, name="z_bf%d" % group, align_bytes=64) for group in range(V // P)]
+        for group in range(LOW // P, V // P):
             cols = slice(group * P, (group + 1) * P)
             nc.vector.tensor_tensor(
-                z_bf[group].rearrange("p (c s u e) -> p c u e s", s=2, u=2, e=2)[:, :, 1],
-                high_terms[0][:, :, cols].rearrange("p e (c s) -> p c e s", s=2),
-                high_terms[1][:, :, cols].rearrange("p e (c s) -> p c e s", s=2),
+                z_bf[group][:].rearrange("p (c s j) -> p c j s", s=2, j=PACK),
+                terms[:, :, 0, cols].rearrange("p j (c s) -> p c j s", s=2),
+                terms[:, :, 1, cols].rearrange("p j (c s) -> p c j s", s=2),
                 ADD,
             )
-        nc.scalar.copy(z_pairs(0), low_back[0][:].rearrange("p u v -> p v u"))
-        last = [keep.tile([P, P // 2 * PACK], BF16, name="z_last%d" % a, align_bytes=64) for a in range(2)]
-        for a in range(2):
+        for group in low_groups:
             nc.scalar.copy(
-                last[a][:].bitcast(F32).rearrange("p (v u) -> p v u", u=2),
-                low_back[1][:, :, a * P // 2 : (a + 1) * P // 2].rearrange("p u v -> p v u"),
+                z_bf[group][:].bitcast(F32).rearrange("p (v u) -> p v u", u=2),
+                back[group][:].rearrange("p u v -> p v u"),
             )
 
-        parts_of_z = [(group * P, P, z_bf[group][:], G_BANKS[group]) for group in (2, 3, 0)]
-        parts_of_z.extend([(P, P // 2, last[0][:], G_BANKS[1]), (P + P // 2, P // 2, last[1][:], 5)])
-        for n, (v0, width, values, bank) in enumerate(parts_of_z):
+        g = keep.tile([P, V], F32, name="g")
+        parts_of_z = [(2 * P, P, 7), (0, P, 2), (P, P, 4), (3 * P, P // 2, 5), (3 * P + P // 2, P // 2, 0)]
+        for n, (v0, width, bank) in enumerate(parts_of_z):
+            values = z_bf[v0 // P][:, v0 % P * PACK : (v0 % P + width) * PACK]
             z_code, z_scale = quantise("z%d" % v0, values, width)
             acc = bank_tile([P, width], "g_acc", bank)
             product(acc[:], w2_code[:], w2_scale[:], z_code[:], z_scale[:])

from contextlib import ExitStack

import concourse.mybir as mybir
from concourse.masks import make_identity

K, T, S, V, H, N, U = 512, 4096, 1024, 512, 512, 128, 256
FLOPS = 2 * K * H * S + 2 * H * N * V

F32 = mybir.dt.float32
BF16 = mybir.dt.bfloat16
I32 = mybir.dt.int32
U32 = mybir.dt.uint32
U16 = mybir.dt.uint16
U8 = mybir.dt.uint8
FP8X4 = mybir.dt.float8_e4m3fn_x4
MULT = mybir.AluOpType.mult
ADD = mybir.AluOpType.add
RELU = mybir.ActivationFunctionType.Relu
COPY = mybir.ActivationFunctionType.Copy

P = 128
PACK = 4
HOPS = 2
STRIPE = 16
QUADRANT = 32
SCALE_STEP = 4
SCALE_FIRST, SCALE_END = 32, 96
SCALE_ROWS = 4
BANK = 512
BLOCK_WORDS = 8

X_LEAD = 1280
X_FIRST = 768
LOW = 256
HIGH = V - LOW
H_WIDTHS = (256, 256, BANK, BANK)
H_BANKS = ((0, 1, 2, 3), (4, 5, 6, 7), (0, 1), (2, 3))
PLAIN_BANKS = (4, 5)
SUM_BANKS = (0, 1)
BACK_BANKS = (3, 6)


def tile_picked_hop2_relu_p_kernel(
    tc, x_words, x_scales, w1, w2, gate, gate2, offs, pos1, pos2, nxt1, nxt2, out
):
    nc = tc.nc
    low_groups = range(LOW // P)
    with ExitStack() as ctx:
        lists = ctx.enter_context(tc.tile_pool(name="lists", bufs=1))
        keep = ctx.enter_context(tc.tile_pool(name="keep", bufs=1))
        psum = ctx.enter_context(tc.psum_pool(name="psum", bufs=1))

        def bank_tile(shape, name, bank):
            return psum.tile(shape, F32, name=name, tag="bank%d" % bank)

        def load_list(name, dram, count):
            tile = lists.tile([P, count // STRIPE], U16, name=name)
            nc.sync.dma_start(tile[:], dram)
            return tile

        def entries(tile, start, count):
            return tile[:, start // STRIPE : (start + count) // STRIPE]

        def quantise(name, values, width):
            code = keep.tile([P, width], U32, name=name + "_code", tag=name + "_code", align_bytes=64)
            scale = keep.tile([P, width], U8, name=name + "_scale", tag=name + "_scale", align_bytes=64)
            nc.vector.quantize_mx(out=code[:].bitcast(FP8X4), scales=scale[:], in_=values)
            return code, scale

        def product(acc, weight_code, weight_scale, moving_code, moving_scale):
            nc.tensor.matmul_mx(
                out=acc,
                lhsT=weight_code.bitcast(FP8X4),
                lhsT_scale=weight_scale,
                rhs=moving_code.bitcast(FP8X4),
                rhs_scale=moving_scale,
                start=True,
                stop=True,
            )

        word_table = keep.tile([P, T], U32, name="word_table", align_bytes=64)
        word_rows = x_words[0].rearrange("p n t -> p (n t)").bitcast(I32)
        nc.sync.dma_start(word_table[:, :X_LEAD].bitcast(I32), word_rows[:, :X_LEAD])
        offs_sb = load_list("offs_sb", offs, S)
        pos_sb = [load_list("pos1_sb", pos1, V)]

        scale_table = keep.tile([P, T], U8, name="scale_table", tag="scale_table", align_bytes=64)
        nc.vector.memset(scale_table[:].bitcast(I32), 0)
        nc.sync.dma_start(scale_table[SCALE_FIRST:SCALE_END:SCALE_STEP, :].bitcast(I32), x_scales[0].bitcast(I32))
        nc.sync.dma_start(word_table[:, X_LEAD:].bitcast(I32), word_rows[:, X_LEAD:])

        w1_rows = w1.rearrange("(p j) c -> p j c", j=PACK)
        half = H // 2
        parts = ((0, half), (half, P), (half + P, P))
        w1_raw = [keep.tile([P, PACK, width], F32, name="w1_raw%d" % c0) for c0, width in parts]

        def load_w1(n):
            nc.sync.dma_start(w1_raw[n][:], w1_rows[:, :, parts[n][0] : parts[n][0] + parts[n][1]])

        load_w1(0)
        load_w1(1)

        x_scale = keep.tile([P, S], U8, name="x_scale", align_bytes=64)
        nc.vector.memset(x_scale[:].bitcast(I32), 0)
        picked_scale = keep.tile([P, S], U8, name="picked_scale", tag="picked", align_bytes=64)
        nc.vector.tensor_copy(picked_scale[:], scale_table[:].indirect(offs_sb[:]))
        for r in range(SCALE_ROWS):
            rows_r = slice(SCALE_FIRST + SCALE_STEP * r, SCALE_END, SCALE_STEP * SCALE_ROWS)
            nc.sync.dma_start(x_scale[r:P:QUADRANT, :].bitcast(I32), picked_scale[rows_r, :].bitcast(I32))
        pos_sb.append(load_list("pos2_sb", pos2, V))
        load_w1(2)

        w2_raw = keep.tile([P, PACK, N], F32, name="w2_raw", align_bytes=64)
        nc.sync.dma_start(w2_raw[:], w2.rearrange("(p j) n -> p j n", j=PACK))
        gate_rows = gate.rearrange("d p v -> p d v")
        gate_sb = keep.tile([P, HOPS, V], F32, name="gate_sb", align_bytes=64)
        nc.sync.dma_start(gate_sb[:, :, LOW:], gate_rows[:, :, LOW:])
        nc.sync.dma_start(gate_sb[:, :, :LOW], gate_rows[:, :, :LOW])
        gate_col = keep.tile([P, HOPS, BLOCK_WORDS], F32, name="gate_col")
        with nc.allow_non_contiguous_dma(reason="one weight a partition"):
            for d in range(HOPS):
                nc.sync.dma_start(gate_col[:, d, : LOW // P], gate[d, 0, :LOW].rearrange("(b v) -> v b", v=P))
        nxt_sb = [load_list("nxt1_sb", nxt1, U), load_list("nxt2_sb", nxt2, U)]
        gate2_sb = keep.tile([P, HOPS, U], F32, name="gate2_sb")
        nc.sync.dma_start(gate2_sb[:], gate2.rearrange("d p u -> p d u"))

        ident = keep.tile([P, P], F32, name="ident", tag="scale_table", align_bytes=64)
        make_identity(nc, ident[:])

        x_first = keep.tile([P, X_FIRST], U32, name="x_first", align_bytes=64)
        nc.vector.tensor_copy(x_first[:], word_table[:].indirect(entries(offs_sb, 0, X_FIRST)))

        w1_high = keep.tile([P, 2, P, PACK], BF16, name="w1_high", align_bytes=64)

        w1_low = [keep.tile([P, P, PACK], BF16, name="w1_low%d" % a, align_bytes=64) for a in range(2)]

        def deal_low(copy, n):
            c0, width = parts[n]
            src = w1_raw[n][:].rearrange("p j (q u e) -> p u q j e", u=2, e=2)[:, 0]
            dst = w1_low[c0 // half][:, c0 % half // 2 : (c0 % half + width) // 2, :]
            copy(dst.rearrange("p (q e) j -> p q j e", e=2), src)

        def deal_high(copy, n):
            c0, width = parts[n]
            src = w1_raw[n][:].rearrange("p j (c s u e) -> p u c j s e", s=2, u=2, e=2)[:, 1]
            dst = w1_high[:, :, c0 // PACK : (c0 + width) // PACK, :]
            copy(dst.rearrange("p e (c s) j -> p c j s e", s=2), src)

        deal_low(nc.scalar.copy, 0)
        code0, scale0 = quantise("w1_0", w1_low[0][:].rearrange("p m j -> p (m j)"), P)
        x_last = keep.tile([P, S - X_FIRST], U32, name="x_last", tag="picked", align_bytes=64)
        nc.vector.tensor_copy(x_last[:], word_table[:].indirect(entries(offs_sb, X_FIRST, S - X_FIRST)))
        deal_high(nc.scalar.copy, 0)
        deal_low(nc.scalar.copy, 1)
        deal_high(nc.scalar.copy, 1)
        deal_low(nc.vector.tensor_copy, 2)
        deal_high(nc.vector.tensor_copy, 2)
        code1, scale1 = quantise("w1_1", w1_low[1][:].rearrange("p m j -> p (m j)"), P)
        w2_bf = keep.tile([P, N, PACK], BF16, name="w2_bf", align_bytes=64)
        nc.vector.tensor_copy(
            w2_bf[:].rearrange("p (c s) j -> p c j s", s=2),
            w2_raw[:].rearrange("p j (c s) -> p c j s", s=2),
        )
        code23, scale23 = quantise("w1_23", w1_high[:].rearrange("p e m j -> p (e m j)"), 2 * P)
        w2_code, w2_scale = quantise("w2", w2_bf[:].rearrange("p n j -> p (n j)"), N)
        w1_code = [code0[:], code1[:], code23[:, :P], code23[:, P:]]
        w1_scale = [scale0[:], scale1[:], scale23[:, :P], scale23[:, P:]]

        h = []

        def x_code(s0, s1):
            return x_first[:, s0:s1] if s0 < X_FIRST else x_last[:, s0 - X_FIRST : s1 - X_FIRST]

        def make_h(t):
            h_t = keep.tile([P, S], F32, name="h%d" % t, align_bytes=64)
            width = H_WIDTHS[t]
            for s0, bank in zip(range(0, S, width), H_BANKS[t]):
                acc = bank_tile([P, width], "h_acc", bank)
                cuts = (s0, X_FIRST, s0 + width) if s0 < X_FIRST < s0 + width else (s0, s0 + width)
                for c0, c1 in zip(cuts, cuts[1:]):
                    product(acc[:, c0 - s0 : c1 - s0], w1_code[t], w1_scale[t], x_code(c0, c1), x_scale[:, c0:c1])
                nc.scalar.activation(h_t[:, s0 : s0 + width], acc[:], RELU)
            h.append(h_t)

        def gather_plain(t, tags):
            tiles = []
            for d in range(HOPS):
                tile = keep.tile([P, LOW], F32, name="plain%d_%d" % (t, d), tag=tags[d], align_bytes=64)
                nc.scalar.activation(tile[:], h[t][:].indirect(entries(pos_sb[d], 0, LOW)), COPY)
                tiles.append(tile)
            return tiles

        make_h(0)
        make_h(1)
        make_h(2)
        plain = [gather_plain(0, ("w1_1_code", "w1_1_scale"))]
        make_h(3)
        plain.append(gather_plain(1, ("plain_first", "plain_second")))


        def gather_terms(dst, t, d, v0, v1):
            nc.vector.tensor_tensor(
                dst, h[t][:].indirect(entries(pos_sb[d], v0, v1 - v0)), gate_sb[:, d, v0:v1], MULT
            )

        terms = keep.tile([P, PACK, HOPS, V], F32, name="terms", align_bytes=64)
        for a in range(2):
            early = keep.tile([P, HOPS, HIGH], F32, name="early%d" % a, align_bytes=64)
            for d in range(HOPS):
                gather_terms(early[:, d, :], a, d, LOW, V)
            for e in range(2):
                nc.sync.dma_start(terms[a * P // 2 : (a + 1) * P // 2, e, :, LOW:], early[e:P:2, :, :])

        plain_turned = [bank_tile([P, HOPS, 2, P], "plain_turned", bank) for bank in PLAIN_BANKS]
        sums = [bank_tile([P, 2, P], "sums", bank) for bank in SUM_BANKS]

        def turn_plain(t):
            for d in range(HOPS):
                for group in low_groups:
                    nc.tensor.transpose(
                        plain_turned[group][:, d, t, :], plain[t][d][:, group * P : (group + 1) * P], ident[:]
                    )

        def sum_terms(t, d):
            for group in low_groups:
                nc.tensor.matmul(
                    sums[group][:, t - 2, :],
                    terms[:, t, d, group * P : (group + 1) * P],
                    ident[:],
                    start=(d == 0),
                    stop=(d == HOPS - 1),
                    is_transpose=True,
                )

        turn_plain(0)
        for d in range(HOPS):
            gather_terms(terms[:, 2, d, :], 2, d, 0, V)
            sum_terms(2, d)
        turn_plain(1)
        for d in range(HOPS):
            gather_terms(terms[:, 3, d, :LOW], 3, d, 0, LOW)
            sum_terms(3, d)
        gather_terms(terms[:, 3, 0, LOW:], 3, 0, LOW, V)
        late = keep.tile([P, HIGH], F32, name="late", align_bytes=64)
        nc.scalar.activation(late[:], h[3][:].indirect(entries(pos_sb[1], LOW, HIGH)), COPY)
        nc.vector.tensor_tensor(terms[:, 3, 1, LOW:], late[:], gate_sb[:, 1, LOW:], MULT)

        def first_pair(group, d):
            return plain_turned[group][:, d].rearrange("v a m -> v (a m)")

        def turn_back(rows, back):
            nc.tensor.transpose(back, rows[:].bitcast(F32), ident[:])

        scaled = []
        for group in low_groups:
            tile = keep.tile([P, 2 * P], F32, name="scaled%d" % group, align_bytes=64)
            nc.scalar.activation(tile[:], first_pair(group, 0), COPY, scale=gate_col[:, 0, group : group + 1])
            scaled.append(tile)
        back = [bank_tile([P, 2, P], "back", bank) for bank in BACK_BANKS]
        for group in low_groups:
            rows = keep.tile([P, 2 * P], BF16, name="rows%d_1" % group, align_bytes=64)
            nc.scalar.copy(rows[:].rearrange("v (p e) -> v p e", e=2), sums[group][:].rearrange("v e p -> v p e"))
            turn_back(rows, back[group][:, 1, :])
        for group in low_groups:
            rows = keep.tile([P, 2 * P], BF16, name="rows%d_0" % group, align_bytes=64)
            nc.vector.scalar_tensor_tensor(
                rows[:], first_pair(group, 1), gate_col[:, 1, group : group + 1], scaled[group][:], MULT, ADD
            )
            turn_back(rows, back[group][:, 0, :])

        z_bf = [keep.tile([P, P * PACK], BF16, name="z_bf%d" % group, align_bytes=64) for group in range(V // P)]
        for group in range(LOW // P, V // P):
            cols = slice(group * P, (group + 1) * P)
            nc.vector.tensor_tensor(
                z_bf[group][:].rearrange("p (c s j) -> p c j s", s=2, j=PACK),
                terms[:, :, 0, cols].rearrange("p j (c s) -> p c j s", s=2),
                terms[:, :, 1, cols].rearrange("p j (c s) -> p c j s", s=2),
                ADD,
            )
        for group in low_groups:
            nc.scalar.copy(
                z_bf[group][:].bitcast(F32).rearrange("p (v u) -> p v u", u=2),
                back[group][:].rearrange("p u v -> p v u"),
            )

        g = keep.tile([P, V], F32, name="g")
        parts_of_z = [(2 * P, P, 7), (0, P, 2), (P, P, 4), (3 * P, P // 2, 5), (3 * P + P // 2, P // 2, 0)]
        for n, (v0, width, bank) in enumerate(parts_of_z):
            values = z_bf[v0 // P][:, v0 % P * PACK : (v0 % P + width) * PACK]
            z_code, z_scale = quantise("z%d" % v0, values, width)
            acc = bank_tile([P, width], "g_acc", bank)
            product(acc[:], w2_code[:], w2_scale[:], z_code[:], z_scale[:])
            cols = g[:, v0 : v0 + width]
            if n == 3:
                nc.vector.tensor_scalar_max(cols, acc[:], 0.0)
            else:
                nc.scalar.activation(cols, acc[:], RELU)

        pieces = [slice(0, U // 2), slice(U // 2, U)]
        second = keep.tile([P, U], F32, name="root_second")
        for cols in pieces:
            nc.scalar.activation(
                second[:, cols], g[:].indirect(entries(nxt_sb[1], cols.start, cols.stop - cols.start)), COPY
            )
        first_term = keep.tile([P, U], F32, name="root_first_term")
        nc.vector.tensor_tensor(first_term[:], g[:].indirect(nxt_sb[0][:]), gate2_sb[:, 0, :], MULT)
        second_term = keep.tile([P, U], F32, name="root_second_term")
        for cols in pieces:
            nc.vector.tensor_tensor(second_term[:, cols], second[:, cols], gate2_sb[:, 1, cols], MULT)
        result = keep.tile([P, U], F32, name="result", align_bytes=64)
        for a, cols in enumerate(pieces):
            nc.vector.tensor_tensor(result[:, cols], first_term[:, cols], second_term[:, cols], ADD)
            nc.sync.dma_start(out[:, cols], result[:, cols])
